import numpy as np, ml_dtypes
CORES = [40,64,80,88,96,104,120,144]
N = 8
import mx_ref
BF = ml_dtypes.bfloat16
def gcols(t, e):
    v = np.concatenate([t.reshape(8, 16, -1, 4), np.zeros((8, 16, 1, 4), BF)], axis=2)
    return np.ascontiguousarray(np.stack([v[g][:, e[g]] for g in range(8)])).reshape(128, -1)
def tile(rs):
    return np.stack(rs, axis=2).reshape(128, -1).astype(BF)
def pick(q, e):
    c = np.concatenate([q[0].reshape(128, -1, 4), np.zeros((128, 1, 4), np.uint8)], axis=1); s = np.concatenate([q[1], np.ones((16, 1), np.uint8)], axis=1)
    return (np.ascontiguousarray(c[:, e].reshape(128, -1)), np.ascontiguousarray(s[:, e]))
def join(*qs):
    return (np.concatenate([q[0] for q in qs], axis=1), np.concatenate([q[1] for q in qs], axis=1))
def put(q, e, v):
    c, s = q[0].reshape(128, -1, 4).copy(), q[1].copy(); c[:, e] = v[0].reshape(128, -1, 4); s[:, e] = v[1]
    return (c.reshape(128, -1), s)
def pk(c, s):
    return (np.ascontiguousarray(c), mx_ref.live(s))
def emit(q):
    return q[0], q[1]
def packed(v, rng):
    q = [mx_ref.quantize(np.ascontiguousarray(v[r])) for r in range(N)]
    return np.stack([a for a, b in q]), np.stack([mx_ref.plane(b, rng) for a, b in q])
def values_of_codes():
    e, c = np.zeros((128, 128, 4), np.float32), np.zeros((128, 2, 4), np.uint8)
    e[np.arange(128), np.arange(128), 0] = 1
    c[:127, :, 0] = np.arange(256).reshape(2, 128).T[:127]
    return mx_ref.matmul(mx_ref.quantize(e.reshape(128, 512).astype(BF)), (c.reshape(128, 8), np.full((16, 2), 127, np.uint8))).T.reshape(-1).astype(np.float64)
CODE_VALUE, SCALE_VALUE = values_of_codes(), 2.0 ** (np.arange(256) - 127.0)
def decode(q):
    return (CODE_VALUE[q[0]].reshape(16, 8, -1, 4) * SCALE_VALUE[q[1]][:, None, :, None] + 0.0).reshape(128, -1).astype(np.float32)
def f(rng, *shape):
    return mx_ref.flush((rng.standard_normal(shape, dtype=np.float32) * np.exp2(rng.integers(-2, 3, shape[:-1] + (1,)))).astype(BF))
def wide(rng, *shape, cols=0):
    v = rng.standard_normal(shape, dtype=np.float32) * np.exp2(rng.integers(-12, 13, shape)).astype(np.float32)
    if cols: v *= np.repeat(np.exp2(rng.integers(-cols, cols + 1, shape[:-2] + (1, shape[-1] // 4))) * (rng.random(shape[:-2] + (1, shape[-1] // 4)) > 0.0625), 4, axis=-1).astype(np.float32)
    return mx_ref.flush(v.astype(BF))
C, K, P, R = 224, 112, 336, 3
ODD = np.arange(1, C, 2)
REFS = np.full((K + 127) // 128 * 128, -1)
REFS[:K] = ODD
def layers(rng):
    return np.array(f(rng, N, 128, 2048)).reshape(N, 8, 16, 4, 8, 16, 4)
def weights(rng, w):
    c, s = packed(np.ascontiguousarray(w).reshape(N, 128, 2048), rng)
    return {"wc": c, "ws": s}
def full(rng, x, w):
    return {"x": np.ascontiguousarray(x).astype(np.float32).reshape(N, 128, 4 * C).astype(BF), "v": np.array(f(rng, N, 128, 512)), **weights(rng, w)}
def apart(rng):
    x = np.array(f(rng, N, 128, 4 * C)).astype(np.float32).reshape(N, 8, 16, C, 4)
    h = rng.permutation(8)[:2]
    x[:, :, :, 1::2] = 0
    x[:, h] = 0
    w = layers(rng)
    w[:, h] = 0
    w[:, :, :, :, h] = 0
    return x, int(h[0]), int(h[1]), w
def setup_inputs(rng):
    return full(rng, np.array(f(rng, N, 128, 4 * C)), layers(rng))
def setup_inputs_ties(rng):
    x, a, b, w = apart(rng)
    x[:, a, :2, ::2] = rng.integers(0, 3, (N, 2, K, 4))
    s = rng.integers(0, 2, (N, 2, K, 4)) * 2.0 ** -8
    s[:, 0, :, 0] = 2.0 ** -8
    x[:, a, :2, 1::2] = s
    for r in range(N):
        k = 2 * int(rng.integers(K)) + 1
        x[r, a, :2, k] = 0
        x[r, a, 0, k, 0] = -2.0 ** -8
    o = rng.permutation(N)
    x[o[0], :, :, 1::2] = 0
    i = [g for g in (2, 4, 6) if g not in (a, b)][0]
    w[o[0], [g for g in range(8) if g != i]] = 0
    x[o[1]] = x[o[1]][:, :, :1].copy()
    return full(rng, x, w)
def setup_inputs_near(rng):
    x, a, b, w = apart(rng)
    c, d = [int(g) for g in rng.permutation(8) if g not in (a, b)][:2]
    x[:, a, 0, ::2, 0] = 1
    x[:, a, 8:12, ::2] = rng.integers(0, 2, (N, 4, K, 4)) * np.exp2(np.arange(4) - 23.0)
    x[:, a, 12, ::2, 0] = 2.0 ** -10
    x[:, b, :4, ::2] = (1 + rng.integers(0, 4, (N, 4, K, 4)) * 0.25) * 2.0 ** -30
    o = rng.permutation(N) % 4
    for r in range(N):
        s = rng.integers(0, 2, (4, K, 4)) * 1.0
        s[0, :, 0] = 1
        if o[r] < 2:
            k = 2.0 ** -8 if o[r] == 0 else 2.0 ** -30
            x[r, a, 0, 1::2, 0] = k
            x[r, a, 12, 1::2, 0] = k
            x[r, a, 8:12, 1::2] = s * k
        else: x[r, b, :4, 1::2] = s * 2.0 ** -30
        if o[r] % 2 == 0: x[r, a, 0, 2 * int(rng.integers(K)), 0] = 2.0 ** 29
    x[:, b, 8, ::2, 0] = 1.96875
    x[:, b, 9:11, ::2] = rng.integers(8, 16, (N, 2, K, 4)) * np.exp2(-13.0 - np.arange(4))
    x[:, :, :, 1:16:2] = 0
    for j in range(8): x[:, b, 9 + j // 4, 2 * j + 1, j % 4] = 1
    x[:, c, :8, ::2] = 0
    x[:, c, 0, ::2, 0] = -3.5
    x[:, d, 8, ::2, :2] = 1
    w[:, :, :, :, d] = 0
    w[:, :, :, :, c, :8] = 0
    w[:, d, 8, :, c, :8, 0] = ((2 * rng.integers(4, 8, (N, 4, 8)) + 1) * np.exp2(-8.0 - np.arange(8) % 4)).astype(np.float32).astype(BF)
    w[:, d, 8, 0, c, 0, 0] = 60
    w[:, d, 8, 0, c, 0, 1] = 3
    return full(rng, x, w)
def setup_inputs_huge(rng):
    x = 0.8 + 0.2 * rng.random((N, 8, 16, C, 4))
    for r in range(N): x[r, :, :, 2 * int(rng.integers(K)) + 1] *= -1.0
    x *= 2.0 ** 30 * float(rng.choice([-1.0, 1.0]))
    w = np.zeros((N, 128, 4, 128, 4), np.float32)
    i = np.arange(128)
    for b in range(4): w[:, i, b, i, b] = -1
    return full(rng, x, w.astype(BF))
def setup_inputs_far(rng):
    x = np.exp2(rng.integers(-14, -7, (N, 16, 8, C, 4))) * (1 + (2 * rng.integers(0, 64, (N, 16, 8, C, 4)) + 1) * 2.0 ** -7) * rng.choice([-1.0, 1.0], (N, 16, 8, C, 4))
    x[:, :, int(rng.integers(8)), :, int(rng.integers(4))] = 1.96875
    x *= np.exp2(-rng.integers(0, 3, (N, 16, 1, C, 1)))
    x *= np.exp2(3.0 * rng.permutation(N))[:, None, None, None, None]
    return full(rng, x, layers(rng))
def setup_inputs_spread(rng):
    return full(rng, wide(rng, N, 128, 4 * C, cols=6), layers(rng))
def check_inputs(d):
    b = []
    for k in ("x", "v"):
        a = np.abs(d[k].astype(np.float32))
        if not (np.isfinite(a).all() and ((a == 0) | (a >= 2.0 ** -30) & (a <= 2.0 ** 30)).all()): b.append("a value of " + k)
    none, least, most = [emit(mx_ref.quantize(np.full((128, 16), k, np.float32).astype(BF)))[1][0, 0] for k in (0.0, 2.0 ** -30, 2.0 ** 30)]
    for r in range(N):
        if ((d["wc"][r] == 0x7F) | (d["wc"][r] == 0xFF)).any(): b.append("wc: a code that is no number")
        s = mx_ref.live(d["ws"][r])
        if ((s != none) & ((s < least) | (s > most))).any(): b.append("ws: a scale out of range")
    return b
def reference(x, v, wc, ws):
    lay = [pk(wc[r], ws[r]) for r in range(N)]
    now = [x[r] for r in range(N)]
    for t in range(R):
        q = [mx_ref.quantize(now[r]) for r in range(N)]
        named, back = [], []
        for r in range(N):
            win = join(q[r], pick(q[(r + 1 + t) % N], np.arange(0, C, 2)))
            s = np.concatenate([mx_ref.matmul(pick(q[r], REFS[i:i + 128]), win) for i in range(0, len(REFS), 128)])[:K] + np.float32(0.0)
            s[np.arange(K), ODD] = -np.inf
            m = np.ascontiguousarray(np.argsort(-s, axis=1, kind="stable")[:, :8].T)
            z = mx_ref.quantize(gcols(decode(win).astype(BF), m))
            h = tile([mx_ref.matmul(pick(lay[r], np.arange(128 * b, 128 * b + 128)), z) * np.float32(0.03125) for b in range(4)])
            named.append(m)
            back.append(mx_ref.quantize(h))
        for r in range(N):
            e = (r - 1 - t) % N
            n = np.full((8, C), -1)
            for k in range(K - 1, -1, -1):
                m = named[e][:, k]
                g = np.nonzero(m >= C)[0]
                n[g, 2 * (m[g] - C)] = K + k
            for k in range(K - 1, -1, -1):
                m = named[r][:, k]
                g = np.nonzero(m < C)[0]
                n[g, m[g]] = k
            a = gcols(decode(join(back[r], back[e])).astype(BF), n)
            now[r] = (decode(q[r]) + a.astype(np.float32)).astype(BF)
    y, op = np.zeros((N, 128, C), np.float32), np.zeros((N, 8, K), np.float32)
    oc, osc = np.zeros((N, 128, 4 * C), np.uint8), np.zeros((N, 16, C), np.uint8)
    for r in range(N):
        last = mx_ref.quantize(now[r])
        y[r] = mx_ref.matmul(mx_ref.quantize(v[r]), last)
        op[r] = named[r]
        oc[r], osc[r] = emit(last)
    return {"y": y, "op": op, "oc": oc, "osc": osc}

@@ -1,0 +1,505 @@
+from concourse.bass import DstId, RemoteDMATransfer
+from concourse.mybir import dt, AluOpType as Alu, ActivationFunctionType as Act
+
+N, C, K, ROUNDS = 8, 224, 112, 3
+W = 368
+RW = 337
+CW = 120
+DW = K + 1
+NS = K + 1 + 8 * C
+UNIT = 4096.0
+BIG = 3.0e29
+SIGNS, LAG = 6, 3
+X4, U8, BF, F32, F16 = "float8_e4m3fn_x4", "uint8", "bfloat16", "float32", "float16"
+
+SCRATCH = {
+    "xin": ("sbuf", [128, 4 * C], BF), "xs": ("sbuf", [128, 1024], BF), "xf": ("sbuf", [128, 4 * C], BF),
+    "vin": ("sbuf", [128, 512], BF), "vq": ("sbuf", [128, 128], X4), "vs": ("sbuf", [128, 128], U8),
+    "wq": ("sbuf", [128, 512], X4), "wp": ("sbuf", [128, 512], U8),
+    "un": ("sbuf", [128, 2048], BF), "eq": ("sbuf", [128, 512], X4), "es": ("sbuf", [128, 512], U8),
+    "fq": ("sbuf", [128, C], X4), "fs": ("sbuf", [128, C], U8), "yo": ("sbuf", [128, C], F32),
+    "vp": ("sbuf", [128, 4 * W], BF), "ep": ("sbuf", [128, 4 * 256], BF),
+    "zt": ("sbuf", [128, 512], BF), "zq": ("sbuf", [128, 128], X4), "zs": ("sbuf", [128, 128], U8),
+    "ht": ("sbuf", [128, 512], BF),
+    "sc": ("sbuf", [128, C], F32), "mk": ("sbuf", [128, K], F32), "big": ("sbuf", [128, C], F32),
+    "rr": ("sbuf", [128, 8 * RW], F32), "cn": ("sbuf", [128, CW], F32),
+    "e1": ("sbuf", [128, 8 * C], BF), "c1": ("sbuf", [128, 8 * C], BF), "s1": ("sbuf", [128, 4 * C], BF),
+    "e2": ("sbuf", [128, 8 * CW], BF), "c2": ("sbuf", [128, 8 * CW], BF), "s2": ("sbuf", [128, 8 * CW], F16),
+    "g1": ("sbuf", [128, 4 * C], BF), "g2": ("sbuf", [128, 8 * CW], BF),
+    "ga": ("sbuf", [128, K], BF),
+    "zer": ("sbuf", [128, 7 * DW], BF), "nj": ("sbuf", [128, 8], BF), "ej": ("sbuf", [128, 8], BF),
+    "mu": ("sbuf", [128, 8], BF), "one": ("sbuf", [128, C], BF),
+    "tb": ("sbuf", [128, 16], F32), "td": ("sbuf", [128, 8], F32), "dl": ("sbuf", [128, CW], F16),
+    "m2": ("sbuf", [128, 32], F32),
+    "mh": ("sbuf", [128, 8], "uint16"), "sl": ("sbuf", [128, NS], BF), "bb": ("sbuf", [128, 128], BF),
+    "tt": ("sbuf", [128, 128], BF), "off": ("sbuf", [128, 8], "uint16"),
+    "idc": ("sbuf", [128, 352], BF), "ll": ("sbuf", [128, K], BF), "idb": ("sbuf", [128, 128], BF),
+    "pi": ("sbuf", [128, 2], "int32"), "pf": ("sbuf", [128, 1], F32), "c22": ("sbuf", [128, 22], F32),
+    "ids": ("sbuf", [128, 22], BF), "nb": ("sbuf", [128, 22], F32),
+    "dd": ("sbuf", [128, 21 * DW], BF), "do": ("sbuf", [128, 21 * DW], BF), "rm": ("sbuf", [128, 7 * DW], BF),
+    "oo": ("sbuf", [128, 8], "uint16"), "oe": ("sbuf", [128, 8], "uint16"), "mn": ("sbuf", [128, 8], F32),
+    "pls": ("sbuf", [128, 352], F32), "opb": ("sbuf", [128, K], F32),
+    "ps": ("psum", [128, 4096], F32),
+}
+for _t in range(ROUNDS):
+    SCRATCH["tq%d" % _t] = ("sbuf", [128, W], X4)
+    SCRATCH["ts%d" % _t] = ("sbuf", [128, W], U8)
+    SCRATCH["hq%d" % _t] = ("sbuf", [128, 240], X4)
+    SCRATCH["hs%d" % _t] = ("sbuf", [128, 240], U8)
+    SCRATCH["lo%d" % _t] = ("sbuf", [128, 8], F32)
+    SCRATCH["li%d" % _t] = ("sbuf", [128, 8], F32)
+
+SEMAPHORES = ["cV", "cA", "cP", "cG", "dx", "dwc", "dws", "dv", "dout", "left"] + \
+    ["a%s%d" % (k, t) for k in "phl" for t in range(ROUNDS)]
+
+
+def bits(engs):
+    return sum(1 << e for e in engs)
+
+
+def routes(T, topo, t, kind, r):
+    src = T.cores[r]
+    dst = T.cores[(r - 1 - t) % N] if kind == "p" else T.cores[(r + 1 + t) % N]
+    q, s, a = ("tq%d" % t, "ts%d" % t, 240) if kind == "p" else ("hq%d" % t, "hs%d" % t, 112)
+
+    def codes(lo, hi):
+        return (lambda: T[q][:, a + lo:a + hi].bitcast(dt.uint8)), (lambda: T[q][:, lo:hi].bitcast(dt.uint8))
+    plane = (lambda: T[s][:, a:a + K]), (lambda: T[s][:, 0:K])
+    lst = (lambda: T["lo%d" % t][:, 0:7]), (lambda: T["li%d" % t][:, 0:7])
+    if topo.may_write(src, dst) and (t, kind) != (0, "p"):
+        e = topo.engines(src, dst)
+        if kind == "l":
+            return dst, [lst + (None, e, None)]
+        return dst, [codes(0, K) + (None, e, None), plane + (None, e, None)]
+    able = [c for c in topo.cores_of(src) if all(topo.may_write(c, d) for d in T.cores)]
+    near = [c for c in able if topo.die(c) == topo.die(src)]
+    far = [c for c in able if topo.die(c) != topo.die(src)]
+    e = topo.engines(src, near[0])
+    h = len(e) // 2
+    if kind == "l":
+        return dst, [lst + (near[1], e, topo.engines(near[1], dst))]
+    return dst, [codes(0, K // 2) + (near[0], e[:h], topo.engines(near[0], dst)),
+                 codes(K // 2, K) + (far[0], e[h:], topo.engines(far[0], dst)),
+                 plane + (near[1], e, topo.engines(near[1], dst))]
+
+
+def landing(T, topo, t, kind, r):
+    s = (r + 1 + t) % N if kind == "p" else (r - 1 - t) % N
+    return sum(len(p[4] if p[2] is not None else p[3]) for p in routes(T, topo, t, kind, s)[1])
+
+
+def relay_program(g, core, T, topo):
+    left = 0
+    for t in range(ROUNDS):
+        for kind in "phl":
+            for r in range(N):
+                dst, pieces = routes(T, topo, t, kind, r)
+                for _, land, via, e1, e2 in pieces:
+                    if via == core:
+                        sem = T.sem["a%s%d" % (kind, t)]
+                        g.wait_ge(sem, len(e1))
+                        rid, pid = topo.addr(dst, core)
+                        g.remote_dma(land(), land(), sem, T.sem.left, pid, rid, bits(e2))
+                        left += len(e2)
+    if left:
+        g.wait_ge(T.sem.left, left)
+
+
+def rank_program(g, core, T, topo):
+    rank = T.rank_of(core)
+    if rank is None:
+        relay_program(g, core, T, topo)
+        return
+    Q = {"V": g.vector, "A": g.scalar, "P": g.tensor, "G": g, "S": g.sync}
+    V, A, P = g.vector, g.scalar, g.tensor
+    total, seen, wrote, readers = {}, {e: {} for e in Q}, {}, {}
+
+    def need(e, r, w):
+        tok = []
+        for k in r:
+            if k in wrote:
+                tok.append(wrote[k])
+            if k.startswith("ps"):
+                tok += [x for x in readers.get(k, []) if x[0] != "c" + e]
+        for k in w:
+            if k in wrote:
+                tok.append(wrote[k])
+            tok += readers.get(k, [])
+        most = {}
+        for s, n in tok:
+            most[s] = max(most.get(s, 0), n)
+        for s, n in most.items():
+            if seen[e].get(s, 0) < n:
+                Q[e].wait_ge(T.sem[s], n)
+                seen[e][s] = n
+
+    def op(e, call, r, w, sem=None):
+        need(e, r, w)
+        s, n = ("c" + e, 1) if sem is None else (sem, 16)
+        call().then_inc(T.sem[s], n)
+        total[s] = total.get(s, 0) + n
+        for k in r:
+            readers.setdefault(k, []).append((s, total[s]))
+        for k in w:
+            wrote[k], readers[k] = (s, total[s]), []
+
+    def send(t, kind, r):
+        need("G", r, [])
+        dst, pieces = routes(T, topo, t, kind, rank)
+        sem = T.sem["a%s%d" % (kind, t)]
+        single = pieces
+        if len(pieces) == 3:
+            tr = []
+            for src, land, via, e1, _ in pieces[:2]:
+                rid, pid = topo.addr(via, core)
+                tr.append(RemoteDMATransfer(dst_ids=[DstId(rid=rid, pnc=pid)], dma_engine_mask=bits(e1), remote_sem=sem,
+                                            src=src(), dst=land()))
+            g.remote_dma_fused(tr, local_sem=T.sem.left)
+            single = pieces[2:]
+        for src, land, via, e1, _ in single:
+            rid, pid = topo.addr(dst if via is None else via, core)
+            g.remote_dma(land(), src(), sem, T.sem.left, pid, rid, bits(e1))
+        total["left"] = total.get("left", 0) + sum(len(p[3]) for p in pieces)
+
+    for t in range(ROUNDS):
+        for kind in "phl":
+            s = "a%s%d" % (kind, t)
+            total[s] = landing(T, topo, t, kind, rank)
+            wrote[s] = (s, total[s])
+
+    def bank(i, a, b):
+        return T.ps[:, 512 * i + a:512 * i + b]
+
+    def mm(i, lq, ls, l0, rq, rs, a, b, r):
+        op("P", lambda: P.matmul_mx(bank(i, 0, b - a), lq[:, l0:l0 + 128], ls[:, l0:l0 + 128], rq[:, a:b], rs[:, a:b],
+                                    True, True), r, ["ps%d" % i])
+
+    def cp(e, out, in_, r, w):
+        if e == "V":
+            op(e, lambda: V.tensor_copy(out, in_), r, w)
+        else:
+            op(e, lambda: A.activation(out, in_, Act.Copy), r, w)
+
+    def fill(ap, c, w):
+        op("V", lambda: V.memset(ap, c), [], w)
+
+    def afill(ap, n, c, w):
+        op("A", lambda: A.activation(ap, T.zer[:, 0:n], Act.Identity, bias=c), ["zer"], w)
+
+    def iota(ap, pat, base, mul, w, whole=False):
+        if whole:
+            op("G", lambda: g.iota(ap, pat, base, mul), [], w)
+        else:
+            op("G", lambda: g.iota(ap, pat, base, mul, allow_small_or_imprecise_dtypes=True), [], w)
+
+    def ts(out, in0, s1, s2, o0, o1, r, w):
+        if o1 is None:
+            op("V", lambda: V.tensor_scalar(out, in0, s1, None, o0), r, w)
+        else:
+            op("V", lambda: V.tensor_scalar(out, in0, s1, s2, o0, o1), r, w)
+
+    def tt(out, in0, in1, o, r, w):
+        op("V", lambda: V.tensor_tensor(out, in0, in1, o), r, w)
+
+    def scan(out, d0, d1, init, o0, o1, r, w):
+        op("V", lambda: V.tensor_tensor_scan(out, d0, d1, init, o0, o1), r, w)
+
+    def quant(q, s, a, b, in_, r, w):
+        op("V", lambda: V.quantize_mx(q[:, a:b], s[:, a:b], in_), r, w)
+
+    def level(k, o, n, d0, r, blk, prev):
+        b = k * RW + o
+        d1 = T.big[:, 0:n] if k == 0 else T.rr[:, b - RW:b - RW + n]
+        rd = r + ["big", "r0"] + ["r%s%d" % (x, k - 1) for x in (blk, prev) if x and k]
+        if prev:
+            rd.append("r%s%d" % (prev, k))
+        scan(T.rr[:, b + 1:b + 1 + n], d0, d1, T.rr[:, b:b + 1], Alu.max, Alu.min, rd, ["r%s%d" % (blk, k)])
+
+    def equal_runs(col, blk):
+        rd = ["r%s%d" % (blk, k) for k in range(8)]
+        yield tt(T.ej[:, 1:8], T.rr[:, RW + col:8 * RW:RW], T.rr[:, col:7 * RW:RW], Alu.is_equal, rd, ["ej"])
+        yield scan(T.nj[:], T.ej[:], T.mu[:], 0.0, Alu.mult, Alu.add, ["ej", "ej0", "mu"], ["nj"])
+
+    def differ(e, seg):
+        c = seg if seg < 14 else seg + 1
+        out = T.dd[:, seg * DW:seg * DW + K]
+        if e == "V":
+            ts(out, T.ll[:], T.ids[:, c:c + 1], 512.0, Alu.not_equal, Alu.mult, ["ll", "ids"], ["dd%d" % seg])
+        else:
+            op("A", lambda: A.activation(out, T.ll[:], Act.Abs, bias=T.nb[:, c:c + 1], scale=512.0),
+               ["ll", "nb"], ["dd%d" % seg])
+
+    def first_hit(blk):
+        a, b = 7 * blk * DW, 7 * (blk + 1) * DW
+        scan(T.do[:, a:b], T.dd[:, a:b], T.rm[:], 4096.0, Alu.min, Alu.add,
+             ["dd%d" % s for s in range(7 * blk, 7 * blk + 7)] + ["ddr", "rm"], ["do%d" % blk])
+
+    def hits(blk):
+        return T.do[:, 7 * blk * DW + K - 1:7 * (blk + 1) * DW:DW]
+
+    op("S", lambda: g.sync.dma_start(T.xin[:], T.x[:]), [], ["xin"], "dx")
+    iota(T.idb[:], [[1, 128]], 0, -1, ["idb"])
+    iota(T.pi[:, 0:1], [[1, 1]], 0, 1, ["pi0"], True)
+    iota(T.c22[:], [[16, 22]], -176, 0, ["c22"])
+    fill(T.zer[:], 0.0, ["zer"])
+    fill(T.xs[:, 448:512], 0.0, ["xpO"])
+    fill(T.xs[:, 960:1024], 0.0, ["xpE"])
+    fill(T.un[:], 0.0, ["un"])
+    afill(T.rr[:, 0:8 * RW:RW], 8, -BIG, ["r0"])
+    afill(T.big[:], C, BIG, ["big"])
+    afill(T.one[:], C, 1.0, ["one"])
+    afill(T.mu[:], 8, -UNIT, ["mu"])
+    afill(T.ej[:, 0:1], 1, 0.0, ["ej0"])
+    afill(T.tb[:, 8:9], 1, float(C), ["tbc"])
+    afill(T.dd[:, K:21 * DW:DW], 21, 512.0, ["ddr"])
+    afill(T.rm[:], 7 * DW, -1.0, ["rm"])
+    for b in range(4):
+        ts(T.un[:, 512 * b + b:512 * b + 512:4], T.idb[:], 0.0, None, Alu.is_equal, None, ["idb", "un"], ["un%d" % b])
+    quant(T.eq, T.es, 0, 512, T.un[:], ["un%d" % b for b in range(4)], ["eq"])
+    op("A", lambda: A.activation(T.mk[:], T.un[:, 0:4 * K:4], Act.Copy, scale=-1.0e29), ["un0"], ["mk"])
+    afill(T.rm[:, K:7 * DW:DW], 7, 4096.0, ["rm"])
+
+    def split(par, base, key):
+        for b in range(4):
+            cp("V", T.xs[:, base + b:base + 448:4], T.xin[:, 4 * par + b:4 * C:8], ["xin"], [key + str(b)])
+
+    XO, XE = ["xO%d" % b for b in range(4)], ["xE%d" % b for b in range(4)]
+    split(0, 512, "xE")
+
+    def odd_block(t, between):
+        tq, tsc = T["tq%d" % t], T["ts%d" % t]
+        quant(tq, tsc, 112, 240, T.xs[:, 0:512], XO + ["xpO"], ["tO%d" % t])
+        mm(4, tq, tsc, 112, tq, tsc, 112, 240, ["tO%d" % t])
+        between()
+        tt(T.sc[:, 1:C:2], bank(4, 0, K), T.mk[:], Alu.add, ["ps4", "mk"], ["scO"])
+
+    def pads():
+        fill(T.zt[:, 448:512], 0.0, ["zp"])
+        fill(T.ht[:, 448:512], 0.0, ["hp"])
+        fill(T.dl[:, 8:CW], 1.0, ["dlc"])
+
+    def even_hit(k):
+        a = (14 + k) * DW
+        scan(T.do[:, a:a + K], T.dd[:, a:a + K], T.rm[:, 0:K], 4096.0, Alu.min, Alu.add,
+             ["dd%d" % (14 + k), "rm"], ["dE%d" % k])
+
+    for t in range(ROUNDS):
+        last = t == ROUNDS - 1
+        tq, tsc, hq, hs = T["tq%d" % t], T["ts%d" % t], T["hq%d" % t], T["hs%d" % t]
+        kO, kE, kP, kH, kG = "tO%d" % t, "tE%d" % t, "ap%d" % t, "hH%d" % t, "ah%d" % t
+        if t == 0:
+            cp("V", T.xs[:, 0:448:4], T.xin[:, 4:4 * C:8], ["xin"], ["xO0"])
+        quant(tq, tsc, 240, W, T.xs[:, 512:1024], XE + ["xpE"], [kE])
+        send(t, "p", [kE])
+        if t == 0:
+            for b in range(1, 4):
+                cp("V", T.xs[:, b:448:4], T.xin[:, 4 + b:4 * C:8], ["xin"], [XO[b]])
+            odd_block(0, pads)
+            iota(T.sl[:, 0:K + 1], [[-1, K + 1]], K - 176, 0, ["sl0"])
+            iota(T.sl[:, K + 1:NS], [[0, 8], [-1, K], [128, 2]], 223 - 176, 0, ["sl1"])
+            iota(T.idc[:], [[1, 352]], -176, 0, ["idc"])
+        else:
+            mm(5, tq, tsc, 112, tq, tsc, 240, W, [kO, kE])
+        if t == 1:
+            iota(T.pls[:, 0:112], [[1, K]], C, 0, ["pl0"])
+            iota(T.pls[:, 112:240], [[2, 128]], 1, 0, ["pl1"])
+            iota(T.pls[:, 240:352], [[2, K]], 0, 0, ["pl2"])
+        mm(6, tq, tsc, 112, tq, tsc, 240, W, [kO, kE])
+        for b in range(4):
+            mm(b, T.eq, T.es, 128 * b, tq, tsc, 112, W, ["eq", kO, kE])
+        cp("A", T.sc[:, 0:C:2], bank(6, 0, K), ["ps6"], ["scE"])
+
+        def own_level(k):
+            if t == 0:
+                level(k, 0, C, T.sc[:], ["scO", "scE"], "E", None)
+            else:
+                level(k, K, K, bank(5, 0, K), ["ps5"], "E", "O")
+
+        def own_sign(k):
+            op("A", lambda: A.activation(T.g1[:, k // 2 * C:(k // 2 + 1) * C], T.sc[:], Act.Sign, scale=-1.0,
+                                         bias=T.rr[:, k * RW + C:k * RW + C + 1]), ["scO", "scE", "rE%d" % k], ["g1%d" % k])
+            b = k // 2
+            cp("A", T.vp[:, W * b + 112:W * b + 352], bank(b, 0, 240), ["ps%d" % b], ["vo%d" % b])
+
+        def own_equal(k):
+            if k % 2:
+                ts(T.e1[:, k * C:(k + 1) * C], T.g1[:, k // 2 * C:(k // 2 + 1) * C], 0.0, UNIT, Alu.is_equal, Alu.mult,
+                   ["g1%d" % k], ["e1%d" % k])
+                return
+            ts(T.e1[:, k * C:(k + 1) * C], T.sc[:], T.rr[:, k * RW + C:k * RW + C + 1], UNIT, Alu.is_equal, Alu.mult,
+               ["scO", "scE", "rE%d" % k], ["e1%d" % k])
+
+        own_level(0)
+        for k in range(1, 8):
+            own_level(k)
+            if k % 2:
+                own_sign(k)
+            own_equal(k - 1)
+        runs = equal_runs(C, "E")
+        next(runs)
+        cp("V", T.cn[:, 0:8], T.rr[:, C:8 * RW:RW], ["rE%d" % k for k in range(8)], ["cn0"])
+        next(runs)
+        own_equal(7)
+        if t == 0:
+            op("S", lambda: g.sync.dma_start(T.wq[:].bitcast(dt.uint8), T.wc[:]), ["e17"], ["wq"], "dwc")
+            op("S", lambda: g.sync.dma_start(T.wp[:], T.ws[:]), [], ["wp"], "dws")
+            op("S", lambda: g.sync.dma_start(T.vin[:], T.v[:]), [], ["vin"], "dv")
+        for k in range(8):
+            seg = T.c1[:, k * C:(k + 1) * C]
+            scan(seg, T.e1[:, k * C:(k + 1) * C], T.zer[:, 0:C], T.nj[:, k:k + 1], Alu.add, Alu.min,
+                 ["e1%d" % k, "zer", "nj"], ["c1%d" % k])
+            if k < 4:
+                op("A", lambda: A.activation(seg, seg, Act.Relu, bias=1.0, accum_out=T.tb[:, k:k + 1]),
+                   ["c1%d" % k], ["tb%d" % k, "c1%d" % k])
+        for k in range(4, 8):
+            scan(T.s1[:, (k - 4) * C:(k - 3) * C], T.c1[:, k * C:(k + 1) * C], T.one[:], -8 * UNIT, Alu.max, Alu.add,
+                 ["c1%d" % k, "one"], ["s1%d" % k])
+        if t == 0:
+            ts(T.pi[:, 1:2], T.pi[:, 0:1], 15, None, Alu.bitwise_and, None, ["pi0"], ["pi1"])
+        cp("V", T.tb[:, 4:8], T.s1[:, C - 1:4 * C:C], ["s14", "s15", "s16", "s17"], ["tb4"])
+        if t == 0:
+            cp("V", T.pf[:], T.pi[:, 1:2], ["pi1"], ["pf"])
+            for b in range(4):
+                fill(T.ep[:, 256 * b + 240:256 * b + 256], 0.0, ["ez%d" % b])
+            ts(T.ids[:], T.c22[:], T.pf[:], None, Alu.add, None, ["c22", "pf"], ["ids"])
+            ts(T.nb[:], T.c22[:], T.pf[:], -512.0, Alu.add, Alu.mult, ["c22", "pf"], ["nb"])
+        if t == 1:
+            quant(T.vq, T.vs, 0, 128, T.vin[:], ["vin"], ["vq"])
+        tt(T.td[:], T.tb[:, 0:8], T.tb[:, 1:9], Alu.subtract, ["tbc"] + ["tb%d" % k for k in range(5)], ["td"])
+        ts(T.dl[:, 0:8], T.td[:], float(C), None, Alu.add, None, ["td"], ["dl"])
+
+        mm(4, tq, tsc, 112, tq, tsc, 0, 128, [kO, kP])
+        mm(7, tq, tsc, 112, tq, tsc, 0, 128, [kO, kP])
+        for b in range(4):
+            mm(b, T.eq, T.es, 128 * b, tq, tsc, 0, 128, ["eq", kO, kP])
+        cp("A", T.cn[:, 8:CW], bank(7, 0, K), ["ps7"], ["cn1"])
+
+        def new_sign(k):
+            op("A", lambda: A.activation(T.g2[:, k * CW:(k + 1) * CW], T.cn[:], Act.Sign, scale=-1.0,
+                                         bias=T.rr[:, k * RW + RW - 1:k * RW + RW]), ["cn0", "cn1", "rP%d" % k], ["g2%d" % k])
+
+        def new_equal(k):
+            if k == 0:
+                ts(T.c2[:, 0:CW], T.g2[:, 0:CW], 0.0, -UNIT, Alu.not_equal, Alu.mult, ["g20"], ["c20"])
+                return
+            if k < SIGNS:
+                ts(T.e2[:, k * CW:(k + 1) * CW], T.g2[:, k * CW:(k + 1) * CW], 0.0, UNIT, Alu.is_equal, Alu.mult,
+                   ["g2%d" % k], ["e2%d" % k])
+                return
+            ts(T.e2[:, k * CW:(k + 1) * CW], T.cn[:], T.rr[:, k * RW + RW - 1:k * RW + RW], UNIT, Alu.is_equal,
+               Alu.mult, ["cn0", "cn1", "rP%d" % k], ["e2%d" % k])
+
+        def count(k):
+            scan(T.c2[:, k * CW:(k + 1) * CW], T.e2[:, k * CW:(k + 1) * CW], T.zer[:, 0:CW], T.nj[:, k:k + 1],
+                 Alu.add, Alu.min, ["e2%d" % k, "zer", "nj"], ["c2%d" % k])
+
+        def name(k):
+            n = 4 * (k % 2) + k // 2
+            scan(T.s2[:, n * CW:(n + 1) * CW], T.c2[:, k * CW:(k + 1) * CW], T.dl[:], -8 * UNIT, Alu.max, Alu.add,
+                 ["c2%d" % k, "dl", "dlc"], ["s2%d" % k])
+
+        for k in range(8):
+            level(k, C, K, bank(4, 0, K), ["ps4"], "P", "E")
+            if k < SIGNS:
+                new_sign(k)
+            if k >= LAG:
+                new_equal(k - LAG)
+        for b in range(4):
+            cp("A", T.vp[:, W * b:W * b + K], bank(b, 0, K), ["ps%d" % b], ["vP%d" % b])
+        runs = equal_runs(RW - 1, "P")
+        new_equal(6)
+        next(runs)
+        new_equal(7)
+        next(runs)
+        for k in range(8 - LAG, 6):
+            new_equal(k)
+        for k in range(1, 8):
+            count(k)
+            name(k - 1)
+        name(7)
+        for a in range(4):
+            cp("V", T.m2[0:32, 8 * a:8 * a + 8], T.s2[32 * a:32 * a + 32, CW - 1:8 * CW:CW],
+               ["s2%d" % k for k in range(8)], ["m2%d" % a])
+        for h in range(4):
+            cp("V", T.mh[32 * h:32 * h + 32, :], T.m2[0:32, h:32:4], ["m20", "m21", "m22", "m23"], ["mh%d" % h])
+        cp("V", T.bb[:], T.sl[:].indirect(T.mh[:]), ["mh0", "mh1", "mh2", "mh3", "sl0", "sl1"], ["bb"])
+        op("V", lambda: V.transpose(T.tt[:], T.bb[:]), ["bb"], ["tt"])
+        ts(T.off[:], T.tt[:, 0:128:16], 176.0, None, Alu.add, None, ["tt"], ["off"])
+        for b in (0, 2, 1, 3):
+            cp("VVAA"[b], T.zt[:, b:448:4], T.vp[:, W * b:W * b + 352].indirect(T.off[:, 0:7]),
+               ["off", "vo%d" % b, "vP%d" % b], ["z%d" % b])
+        cp("A", T.ll[:], T.idc[:].indirect(T.off[:, 0:7]), ["off", "idc"], ["ll"])
+        quant(T.zq, T.zs, 0, 128, T.zt[:], ["z0", "z1", "z2", "z3", "zp"], ["zq"])
+        for b in (0, 2, 1, 3):
+            mm(4 + b, T.wq, T.wp, 128 * b, T.zq, T.zs, 0, 128, ["wq", "wp", "zq"])
+        for s in range(3):
+            differ("V", s)
+        for b in (0, 2, 1, 3):
+            if b < 2:
+                ts(T.ht[:, b:448:4], bank(4 + b, 0, K), 0.03125, None, Alu.mult, None, ["ps%d" % (4 + b)], ["h%d" % b])
+            else:
+                op("A", lambda: A.activation(T.ht[:, b:448:4], bank(4 + b, 0, K), Act.Copy, scale=0.03125),
+                   ["ps%d" % (4 + b)], ["h%d" % b])
+        differ("V", 3)
+        differ("A", 6)
+        quant(hq, hs, 112, 240, T.ht[:], ["h0", "h1", "h2", "h3", "hp"], [kH])
+        send(t, "h", [kH])
+        for b in range(4):
+            mm(b, T.eq, T.es, 128 * b, hq, hs, 112, 240, ["eq", kH])
+        for s in range(4, 6):
+            differ("V", s)
+        for s in range(7, 11):
+            differ("A", s)
+        first_hit(0)
+        differ("V", 11)
+        ts(T["lo%d" % t][:, 0:7], hits(0), 0.0, 128.0, Alu.min, Alu.add, ["do0"], ["lo%d" % t])
+        send(t, "l", ["lo%d" % t])
+        differ("V", 12)
+        differ("V", 13)
+        for b in range(4):
+            cp("A", T.ep[:, 256 * b:256 * b + 128], bank(b, 0, 128), ["ps%d" % b], ["eo%d" % b])
+        first_hit(1)
+        for s in range(14, 21):
+            differ("A", s)
+        ts(T.oo[:, 0:7], hits(1), 0.0, 112.0, Alu.min, Alu.add, ["do1"], ["oo"])
+        for b in range(4):
+            out = T.xf[:, 4 + b:4 * C:8] if last else T.xs[:, b:448:4]
+            tt(out, T.ep[:, 256 * b:256 * b + 128].indirect(T.oo[:, 0:7]), T.vp[:, W * b + 112:W * b + 224], Alu.add,
+               ["oo", "eo%d" % b, "vo%d" % b], [XO[b]])
+        if last:
+            cp("A", T.opb[:], T.pls[:].indirect(T.off[:, 0:7]), ["off", "pl0", "pl1", "pl2"], ["opb"])
+            for k in range(8):
+                op("S", lambda: g.sync.dma_start(T.op[k:k + 1, :], T.opb[16 * k:16 * k + 1, :]), ["opb"], [], "dout")
+            first_hit(2)
+        else:
+            odd_block(t + 1, lambda: [even_hit(0), even_hit(1)])
+            for k in range(8):
+                level(k, 0, K, T.sc[:, 1:C:2], ["scO"], "O", None)
+                if k < 5:
+                    even_hit(k + 2)
+        mm(5, T.eq, T.es, 384, tq, tsc, 240, W, ["eq", kE])
+        for b in range(4):
+            mm(b, T.eq, T.es, 128 * b, hq, hs, 0, 128, ["eq", kH, kG])
+        for b in range(4):
+            cp("A", T.ep[:, 256 * b + 128:256 * b + 240], bank(b, 0, K), ["ps%d" % b], ["eg%d" % b])
+        tt(T.mn[:, 0:7], hits(2), T["li%d" % t][:, 0:7], Alu.min,
+           ["do2", "al%d" % t] + ["dE%d" % k for k in range(7)], ["mn"])
+        ts(T.oe[:, 0:7], T.mn[:, 0:7], 112.0, None, Alu.add, None, ["mn"], ["oe"])
+        cp("A", T.ga[:], T.ep[:, 768:1024].indirect(T.oe[:, 0:7]), ["oe", "eo3", "eg3", "ez3"], ["ga"])
+        for b in range(4):
+            out = T.xf[:, b:4 * C:8] if last else T.xs[:, 512 + b:960:4]
+            if b == 3:
+                tt(out, T.ga[:], bank(5, 0, K), Alu.add, ["ga", "ps5"], [XE[b]])
+                continue
+            tt(out, T.ep[:, 256 * b:256 * b + 256].indirect(T.oe[:, 0:7]), T.vp[:, W * b + 240:W * b + 352], Alu.add,
+               ["oe", "eo%d" % b, "eg%d" % b, "ez%d" % b, "vo%d" % b], [XE[b]])
+
+    quant(T.fq, T.fs, 0, C, T.xf[:], XO + XE, ["fq"])
+    mm(4, T.vq, T.vs, 0, T.fq, T.fs, 0, C, ["vq", "fq"])
+    op("S", lambda: g.sync.dma_start(T.oc[:], T.fq[:].bitcast(dt.uint8)), ["fq"], [], "dout")
+    for k in range(4):
+        op("A", lambda: A.dma_start(T.osc[4 * k:4 * k + 4, :], T.fs[32 * k:32 * k + 4, :]), ["fq"], [], "dout")
+    cp("V", T.yo[:], bank(4, 0, C), ["ps4"], ["yo"])
+    op("S", lambda: g.sync.dma_start(T.y[:], T.yo[:]), ["yo"], [], "dout")
+    for s, n in total.items():
+        g.wait_ge(T.sem[s], n)

@@ -1,4 +1,3 @@
-from concourse.bass import DstId, RemoteDMATransfer
 from concourse.mybir import dt, AluOpType as Alu, ActivationFunctionType as Act
 
 N, C, K, ROUNDS = 8, 224, 112, 3
@@ -9,7 +8,6 @@ DW = K + 1
 NS = K + 1 + 8 * C
 UNIT = 4096.0
 BIG = 3.0e29
-SIGNS, LAG = 6, 3
 X4, U8, BF, F32, F16 = "float8_e4m3fn_x4", "uint8", "bfloat16", "float32", "float16"
 
 SCRATCH = {
@@ -25,7 +23,6 @@ SCRATCH = {
     "rr": ("sbuf", [128, 8 * RW], F32), "cn": ("sbuf", [128, CW], F32),
     "e1": ("sbuf", [128, 8 * C], BF), "c1": ("sbuf", [128, 8 * C], BF), "s1": ("sbuf", [128, 4 * C], BF),
     "e2": ("sbuf", [128, 8 * CW], BF), "c2": ("sbuf", [128, 8 * CW], BF), "s2": ("sbuf", [128, 8 * CW], F16),
-    "g1": ("sbuf", [128, 4 * C], BF), "g2": ("sbuf", [128, 8 * CW], BF),
     "ga": ("sbuf", [128, K], BF),
     "zer": ("sbuf", [128, 7 * DW], BF), "nj": ("sbuf", [128, 8], BF), "ej": ("sbuf", [128, 8], BF),
     "mu": ("sbuf", [128, 8], BF), "one": ("sbuf", [128, C], BF),
@@ -61,26 +58,21 @@ def routes(T, topo, t, kind, r):
     src = T.cores[r]
     dst = T.cores[(r - 1 - t) % N] if kind == "p" else T.cores[(r + 1 + t) % N]
     q, s, a = ("tq%d" % t, "ts%d" % t, 240) if kind == "p" else ("hq%d" % t, "hs%d" % t, 112)
-
-    def codes(lo, hi):
-        return (lambda: T[q][:, a + lo:a + hi].bitcast(dt.uint8)), (lambda: T[q][:, lo:hi].bitcast(dt.uint8))
+    codes = (lambda: T[q][:, a:a + K].bitcast(dt.uint8)), (lambda: T[q][:, 0:K].bitcast(dt.uint8))
     plane = (lambda: T[s][:, a:a + K]), (lambda: T[s][:, 0:K])
     lst = (lambda: T["lo%d" % t][:, 0:7]), (lambda: T["li%d" % t][:, 0:7])
     if topo.may_write(src, dst) and (t, kind) != (0, "p"):
         e = topo.engines(src, dst)
         if kind == "l":
             return dst, [lst + (None, e, None)]
-        return dst, [codes(0, K) + (None, e, None), plane + (None, e, None)]
+        return dst, [codes + (None, e, None), plane + (None, e, None)]
     able = [c for c in topo.cores_of(src) if all(topo.may_write(c, d) for d in T.cores)]
-    near = [c for c in able if topo.die(c) == topo.die(src)]
-    far = [c for c in able if topo.die(c) != topo.die(src)]
-    e = topo.engines(src, near[0])
-    h = len(e) // 2
+    near = [c for c in able if topo.die(c) == topo.die(src)][0]
+    far = [c for c in able if topo.die(c) != topo.die(src)][0]
+    e = topo.engines(src, near)
     if kind == "l":
-        return dst, [lst + (near[1], e, topo.engines(near[1], dst))]
-    return dst, [codes(0, K // 2) + (near[0], e[:h], topo.engines(near[0], dst)),
-                 codes(K // 2, K) + (far[0], e[h:], topo.engines(far[0], dst)),
-                 plane + (near[1], e, topo.engines(near[1], dst))]
+        return dst, [lst + (far, e, topo.engines(far, dst))]
+    return dst, [codes + (near, e, topo.engines(near, dst)), plane + (far, e, topo.engines(far, dst))]
 
 
 def landing(T, topo, t, kind, r):
@@ -146,19 +138,9 @@ def rank_program(g, core, T, topo):
     def send(t, kind, r):
         need("G", r, [])
         dst, pieces = routes(T, topo, t, kind, rank)
-        sem = T.sem["a%s%d" % (kind, t)]
-        single = pieces
-        if len(pieces) == 3:
-            tr = []
-            for src, land, via, e1, _ in pieces[:2]:
-                rid, pid = topo.addr(via, core)
-                tr.append(RemoteDMATransfer(dst_ids=[DstId(rid=rid, pnc=pid)], dma_engine_mask=bits(e1), remote_sem=sem,
-                                            src=src(), dst=land()))
-            g.remote_dma_fused(tr, local_sem=T.sem.left)
-            single = pieces[2:]
-        for src, land, via, e1, _ in single:
+        for src, land, via, e1, _ in pieces:
             rid, pid = topo.addr(dst if via is None else via, core)
-            g.remote_dma(land(), src(), sem, T.sem.left, pid, rid, bits(e1))
+            g.remote_dma(land(), src(), T.sem["a%s%d" % (kind, t)], T.sem.left, pid, rid, bits(e1))
         total["left"] = total.get("left", 0) + sum(len(p[3]) for p in pieces)
 
     for t in range(ROUNDS):
@@ -253,18 +235,19 @@ def rank_program(g, core, T, topo):
     afill(T.tb[:, 8:9], 1, float(C), ["tbc"])
     afill(T.dd[:, K:21 * DW:DW], 21, 512.0, ["ddr"])
     afill(T.rm[:], 7 * DW, -1.0, ["rm"])
+    fill(T.zt[:, 448:512], 0.0, ["zp"])
+    fill(T.ht[:, 448:512], 0.0, ["hp"])
+    fill(T.dl[:, 8:CW], 1.0, ["dlc"])
     for b in range(4):
         ts(T.un[:, 512 * b + b:512 * b + 512:4], T.idb[:], 0.0, None, Alu.is_equal, None, ["idb", "un"], ["un%d" % b])
-    quant(T.eq, T.es, 0, 512, T.un[:], ["un%d" % b for b in range(4)], ["eq"])
     op("A", lambda: A.activation(T.mk[:], T.un[:, 0:4 * K:4], Act.Copy, scale=-1.0e29), ["un0"], ["mk"])
     afill(T.rm[:, K:7 * DW:DW], 7, 4096.0, ["rm"])
 
-    def split(par, base, key):
-        for b in range(4):
-            cp("V", T.xs[:, base + b:base + 448:4], T.xin[:, 4 * par + b:4 * C:8], ["xin"], [key + str(b)])
-
     XO, XE = ["xO%d" % b for b in range(4)], ["xE%d" % b for b in range(4)]
-    split(0, 512, "xE")
+    for b in range(4):
+        cp("V", T.xs[:, 512 + b:960:4], T.xin[:, b:4 * C:8], ["xin"], [XE[b]])
+    for b in range(4):
+        cp("V", T.xs[:, b:448:4], T.xin[:, 4 + b:4 * C:8], ["xin"], [XO[b]])
 
     def odd_block(t, between):
         tq, tsc = T["tq%d" % t], T["ts%d" % t]
@@ -273,41 +256,39 @@ def rank_program(g, core, T, topo):
         between()
         tt(T.sc[:, 1:C:2], bank(4, 0, K), T.mk[:], Alu.add, ["ps4", "mk"], ["scO"])
 
-    def pads():
-        fill(T.zt[:, 448:512], 0.0, ["zp"])
-        fill(T.ht[:, 448:512], 0.0, ["hp"])
-        fill(T.dl[:, 8:CW], 1.0, ["dlc"])
-
-    def even_hit(k):
-        a = (14 + k) * DW
-        scan(T.do[:, a:a + K], T.dd[:, a:a + K], T.rm[:, 0:K], 4096.0, Alu.min, Alu.add,
-             ["dd%d" % (14 + k), "rm"], ["dE%d" % k])
+    def odd_level(k):
+        level(k, 0, K, T.sc[:, 1:C:2], ["scO"], "O", None)
 
     for t in range(ROUNDS):
         last = t == ROUNDS - 1
         tq, tsc, hq, hs = T["tq%d" % t], T["ts%d" % t], T["hq%d" % t], T["hs%d" % t]
         kO, kE, kP, kH, kG = "tO%d" % t, "tE%d" % t, "ap%d" % t, "hH%d" % t, "ah%d" % t
-        if t == 0:
-            cp("V", T.xs[:, 0:448:4], T.xin[:, 4:4 * C:8], ["xin"], ["xO0"])
         quant(tq, tsc, 240, W, T.xs[:, 512:1024], XE + ["xpE"], [kE])
         send(t, "p", [kE])
         if t == 0:
-            for b in range(1, 4):
-                cp("V", T.xs[:, b:448:4], T.xin[:, 4 + b:4 * C:8], ["xin"], [XO[b]])
-            odd_block(0, pads)
+            odd_block(0, lambda: quant(T.eq, T.es, 0, 512, T.un[:], ["un%d" % b for b in range(4)], ["eq"]))
             iota(T.sl[:, 0:K + 1], [[-1, K + 1]], K - 176, 0, ["sl0"])
             iota(T.sl[:, K + 1:NS], [[0, 8], [-1, K], [128, 2]], 223 - 176, 0, ["sl1"])
             iota(T.idc[:], [[1, 352]], -176, 0, ["idc"])
         else:
             mm(5, tq, tsc, 112, tq, tsc, 240, W, [kO, kE])
+            odd_level(7)
         if t == 1:
             iota(T.pls[:, 0:112], [[1, K]], C, 0, ["pl0"])
             iota(T.pls[:, 112:240], [[2, 128]], 1, 0, ["pl1"])
             iota(T.pls[:, 240:352], [[2, K]], 0, 0, ["pl2"])
+            quant(T.vq, T.vs, 0, 128, T.vin[:], ["vin"], ["vq"])
         mm(6, tq, tsc, 112, tq, tsc, 240, W, [kO, kE])
         for b in range(4):
             mm(b, T.eq, T.es, 128 * b, tq, tsc, 112, W, ["eq", kO, kE])
         cp("A", T.sc[:, 0:C:2], bank(6, 0, K), ["ps6"], ["scE"])
+        for b in range(4):
+            cp("A", T.vp[:, W * b + 112:W * b + 352], bank(b, 0, 240), ["ps%d" % b], ["vo%d" % b])
+        if t == 0:
+            ts(T.pi[:, 1:2], T.pi[:, 0:1], 15, None, Alu.bitwise_and, None, ["pi0"], ["pi1"])
+            for b in range(4):
+                fill(T.ep[:, 256 * b + 240:256 * b + 256], 0.0, ["ez%d" % b])
+            cp("V", T.pf[:], T.pi[:, 1:2], ["pi1"], ["pf"])
 
         def own_level(k):
             if t == 0:
@@ -315,79 +296,58 @@ def rank_program(g, core, T, topo):
             else:
                 level(k, K, K, bank(5, 0, K), ["ps5"], "E", "O")
 
-        def own_sign(k):
-            op("A", lambda: A.activation(T.g1[:, k // 2 * C:(k // 2 + 1) * C], T.sc[:], Act.Sign, scale=-1.0,
-                                         bias=T.rr[:, k * RW + C:k * RW + C + 1]), ["scO", "scE", "rE%d" % k], ["g1%d" % k])
-            b = k // 2
-            cp("A", T.vp[:, W * b + 112:W * b + 352], bank(b, 0, 240), ["ps%d" % b], ["vo%d" % b])
-
         def own_equal(k):
-            if k % 2:
-                ts(T.e1[:, k * C:(k + 1) * C], T.g1[:, k // 2 * C:(k // 2 + 1) * C], 0.0, UNIT, Alu.is_equal, Alu.mult,
-                   ["g1%d" % k], ["e1%d" % k])
-                return
             ts(T.e1[:, k * C:(k + 1) * C], T.sc[:], T.rr[:, k * RW + C:k * RW + C + 1], UNIT, Alu.is_equal, Alu.mult,
                ["scO", "scE", "rE%d" % k], ["e1%d" % k])
 
-        own_level(0)
-        for k in range(1, 8):
-            own_level(k)
-            if k % 2:
-                own_sign(k)
-            own_equal(k - 1)
-        runs = equal_runs(C, "E")
-        next(runs)
-        cp("V", T.cn[:, 0:8], T.rr[:, C:8 * RW:RW], ["rE%d" % k for k in range(8)], ["cn0"])
-        next(runs)
-        own_equal(7)
-        if t == 0:
-            op("S", lambda: g.sync.dma_start(T.wq[:].bitcast(dt.uint8), T.wc[:]), ["e17"], ["wq"], "dwc")
-            op("S", lambda: g.sync.dma_start(T.wp[:], T.ws[:]), [], ["wp"], "dws")
-            op("S", lambda: g.sync.dma_start(T.vin[:], T.v[:]), [], ["vin"], "dv")
-        for k in range(8):
+        def own_count(k):
             seg = T.c1[:, k * C:(k + 1) * C]
             scan(seg, T.e1[:, k * C:(k + 1) * C], T.zer[:, 0:C], T.nj[:, k:k + 1], Alu.add, Alu.min,
                  ["e1%d" % k, "zer", "nj"], ["c1%d" % k])
             if k < 4:
                 op("A", lambda: A.activation(seg, seg, Act.Relu, bias=1.0, accum_out=T.tb[:, k:k + 1]),
                    ["c1%d" % k], ["tb%d" % k, "c1%d" % k])
-        for k in range(4, 8):
+
+        def own_name(k):
             scan(T.s1[:, (k - 4) * C:(k - 3) * C], T.c1[:, k * C:(k + 1) * C], T.one[:], -8 * UNIT, Alu.max, Alu.add,
                  ["c1%d" % k, "one"], ["s1%d" % k])
+
+        own_level(0)
         if t == 0:
-            ts(T.pi[:, 1:2], T.pi[:, 0:1], 15, None, Alu.bitwise_and, None, ["pi0"], ["pi1"])
-        cp("V", T.tb[:, 4:8], T.s1[:, C - 1:4 * C:C], ["s14", "s15", "s16", "s17"], ["tb4"])
-        if t == 0:
-            cp("V", T.pf[:], T.pi[:, 1:2], ["pi1"], ["pf"])
-            for b in range(4):
-                fill(T.ep[:, 256 * b + 240:256 * b + 256], 0.0, ["ez%d" % b])
             ts(T.ids[:], T.c22[:], T.pf[:], None, Alu.add, None, ["c22", "pf"], ["ids"])
             ts(T.nb[:], T.c22[:], T.pf[:], -512.0, Alu.add, Alu.mult, ["c22", "pf"], ["nb"])
-        if t == 1:
-            quant(T.vq, T.vs, 0, 128, T.vin[:], ["vin"], ["vq"])
-        tt(T.td[:], T.tb[:, 0:8], T.tb[:, 1:9], Alu.subtract, ["tbc"] + ["tb%d" % k for k in range(5)], ["td"])
-        ts(T.dl[:, 0:8], T.td[:], float(C), None, Alu.add, None, ["td"], ["dl"])
+        own_level(1)
+        for k in range(2, 8):
+            own_equal(k - 2)
+            own_level(k)
+        runs = equal_runs(C, "E")
+        own_equal(6)
+        next(runs)
+        own_equal(7)
+        next(runs)
+        cp("V", T.cn[:, 0:8], T.rr[:, C:8 * RW:RW], ["rE%d" % k for k in range(8)], ["cn0"])
+        if t == 0:
+            op("S", lambda: g.sync.dma_start(T.wq[:].bitcast(dt.uint8), T.wc[:]), ["e17"], ["wq"], "dwc")
+            op("S", lambda: g.sync.dma_start(T.wp[:], T.ws[:]), [], ["wp"], "dws")
+            op("S", lambda: g.sync.dma_start(T.vin[:], T.v[:]), [], ["vin"], "dv")
+        for k in range(5):
+            own_count(k)
 
         mm(4, tq, tsc, 112, tq, tsc, 0, 128, [kO, kP])
         mm(7, tq, tsc, 112, tq, tsc, 0, 128, [kO, kP])
         for b in range(4):
             mm(b, T.eq, T.es, 128 * b, tq, tsc, 0, 128, ["eq", kO, kP])
         cp("A", T.cn[:, 8:CW], bank(7, 0, K), ["ps7"], ["cn1"])
-
-        def new_sign(k):
-            op("A", lambda: A.activation(T.g2[:, k * CW:(k + 1) * CW], T.cn[:], Act.Sign, scale=-1.0,
-                                         bias=T.rr[:, k * RW + RW - 1:k * RW + RW]), ["cn0", "cn1", "rP%d" % k], ["g2%d" % k])
+        for b in range(4):
+            cp("A", T.vp[:, W * b:W * b + K], bank(b, 0, K), ["ps%d" % b], ["vP%d" % b])
 
         def new_equal(k):
+            best = T.rr[:, k * RW + RW - 1:k * RW + RW]
             if k == 0:
-                ts(T.c2[:, 0:CW], T.g2[:, 0:CW], 0.0, -UNIT, Alu.not_equal, Alu.mult, ["g20"], ["c20"])
-                return
-            if k < SIGNS:
-                ts(T.e2[:, k * CW:(k + 1) * CW], T.g2[:, k * CW:(k + 1) * CW], 0.0, UNIT, Alu.is_equal, Alu.mult,
-                   ["g2%d" % k], ["e2%d" % k])
-                return
-            ts(T.e2[:, k * CW:(k + 1) * CW], T.cn[:], T.rr[:, k * RW + RW - 1:k * RW + RW], UNIT, Alu.is_equal,
-               Alu.mult, ["cn0", "cn1", "rP%d" % k], ["e2%d" % k])
+                ts(T.c2[:, 0:CW], T.cn[:], best, -UNIT, Alu.not_equal, Alu.mult, ["cn0", "cn1", "rP0"], ["c20"])
+            else:
+                ts(T.e2[:, k * CW:(k + 1) * CW], T.cn[:], best, UNIT, Alu.is_equal, Alu.mult,
+                   ["cn0", "cn1", "rP%d" % k], ["e2%d" % k])
 
         def count(k):
             scan(T.c2[:, k * CW:(k + 1) * CW], T.e2[:, k * CW:(k + 1) * CW], T.zer[:, 0:CW], T.nj[:, k:k + 1],
@@ -398,25 +358,28 @@ def rank_program(g, core, T, topo):
             scan(T.s2[:, n * CW:(n + 1) * CW], T.c2[:, k * CW:(k + 1) * CW], T.dl[:], -8 * UNIT, Alu.max, Alu.add,
                  ["c2%d" % k, "dl", "dlc"], ["s2%d" % k])
 
+        def own_tail():
+            cp("V", T.tb[:, 4:8], T.s1[:, C - 1:4 * C:C], ["s14", "s15", "s16", "s17"], ["tb4"])
+
+        def steps():
+            tt(T.td[:], T.tb[:, 0:8], T.tb[:, 1:9], Alu.subtract, ["tbc"] + ["tb%d" % k for k in range(5)], ["td"])
+
+        def steps_on():
+            ts(T.dl[:, 0:8], T.td[:], float(C), None, Alu.add, None, ["td"], ["dl"])
+
+        runs = equal_runs(RW - 1, "P")
+        between = [[(own_count, 5), (own_count, 6)], [(own_count, 7), (own_name, 4)], [(own_name, 5), (own_name, 6)],
+                   [(own_name, 7), (new_equal, 0)], [(new_equal, 1), (own_tail,), (new_equal, 2)],
+                   [(new_equal, 3), (steps,)], [(new_equal, 4), (steps_on,)],
+                   [(new_equal, 5), (new_equal, 6), (next, runs), (name, 0), (new_equal, 7), (next, runs)]]
         for k in range(8):
             level(k, C, K, bank(4, 0, K), ["ps4"], "P", "E")
-            if k < SIGNS:
-                new_sign(k)
-            if k >= LAG:
-                new_equal(k - LAG)
-        for b in range(4):
-            cp("A", T.vp[:, W * b:W * b + K], bank(b, 0, K), ["ps%d" % b], ["vP%d" % b])
-        runs = equal_runs(RW - 1, "P")
-        new_equal(6)
-        next(runs)
-        new_equal(7)
-        next(runs)
-        for k in range(8 - LAG, 6):
-            new_equal(k)
+            for call in between[k]:
+                call[0](*call[1:])
         for k in range(1, 8):
             count(k)
-            name(k - 1)
-        name(7)
+        for k in range(1, 8):
+            name(k)
         for a in range(4):
             cp("V", T.m2[0:32, 8 * a:8 * a + 8], T.s2[32 * a:32 * a + 32, CW - 1:8 * CW:CW],
                ["s2%d" % k for k in range(8)], ["m2%d" % a])
@@ -428,71 +391,71 @@ def rank_program(g, core, T, topo):
         for b in (0, 2, 1, 3):
             cp("VVAA"[b], T.zt[:, b:448:4], T.vp[:, W * b:W * b + 352].indirect(T.off[:, 0:7]),
                ["off", "vo%d" % b, "vP%d" % b], ["z%d" % b])
-        cp("A", T.ll[:], T.idc[:].indirect(T.off[:, 0:7]), ["off", "idc"], ["ll"])
+        cp("V", T.ll[:], T.idc[:].indirect(T.off[:, 0:7]), ["off", "idc"], ["ll"])
         quant(T.zq, T.zs, 0, 128, T.zt[:], ["z0", "z1", "z2", "z3", "zp"], ["zq"])
         for b in (0, 2, 1, 3):
             mm(4 + b, T.wq, T.wp, 128 * b, T.zq, T.zs, 0, 128, ["wq", "wp", "zq"])
-        for s in range(3):
+        for s in range(7):
             differ("V", s)
+        for s in range(7, 9):
+            differ("A", s)
         for b in (0, 2, 1, 3):
             if b < 2:
                 ts(T.ht[:, b:448:4], bank(4 + b, 0, K), 0.03125, None, Alu.mult, None, ["ps%d" % (4 + b)], ["h%d" % b])
             else:
                 op("A", lambda: A.activation(T.ht[:, b:448:4], bank(4 + b, 0, K), Act.Copy, scale=0.03125),
                    ["ps%d" % (4 + b)], ["h%d" % b])
-        differ("V", 3)
-        differ("A", 6)
+        first_hit(0)
         quant(hq, hs, 112, 240, T.ht[:], ["h0", "h1", "h2", "h3", "hp"], [kH])
         send(t, "h", [kH])
         for b in range(4):
             mm(b, T.eq, T.es, 128 * b, hq, hs, 112, 240, ["eq", kH])
-        for s in range(4, 6):
-            differ("V", s)
-        for s in range(7, 11):
-            differ("A", s)
-        first_hit(0)
-        differ("V", 11)
         ts(T["lo%d" % t][:, 0:7], hits(0), 0.0, 128.0, Alu.min, Alu.add, ["do0"], ["lo%d" % t])
         send(t, "l", ["lo%d" % t])
-        differ("V", 12)
-        differ("V", 13)
+        for s in range(9, 12):
+            differ("A", s)
+        for s in (12, 13, 14, 15, 16, 17):
+            differ("V", s)
         for b in range(4):
             cp("A", T.ep[:, 256 * b:256 * b + 128], bank(b, 0, 128), ["ps%d" % b], ["eo%d" % b])
         first_hit(1)
-        for s in range(14, 21):
-            differ("A", s)
+        for s in (18, 19, 20):
+            differ("V", s)
         ts(T.oo[:, 0:7], hits(1), 0.0, 112.0, Alu.min, Alu.add, ["do1"], ["oo"])
+        first_hit(2)
         for b in range(4):
             out = T.xf[:, 4 + b:4 * C:8] if last else T.xs[:, b:448:4]
             tt(out, T.ep[:, 256 * b:256 * b + 128].indirect(T.oo[:, 0:7]), T.vp[:, W * b + 112:W * b + 224], Alu.add,
                ["oo", "eo%d" % b, "vo%d" % b], [XO[b]])
+        mm(5, T.eq, T.es, 384, tq, tsc, 240, W, ["eq", kE])
         if last:
             cp("A", T.opb[:], T.pls[:].indirect(T.off[:, 0:7]), ["off", "pl0", "pl1", "pl2"], ["opb"])
             for k in range(8):
                 op("S", lambda: g.sync.dma_start(T.op[k:k + 1, :], T.opb[16 * k:16 * k + 1, :]), ["opb"], [], "dout")
-            first_hit(2)
         else:
-            odd_block(t + 1, lambda: [even_hit(0), even_hit(1)])
-            for k in range(8):
-                level(k, 0, K, T.sc[:, 1:C:2], ["scO"], "O", None)
-                if k < 5:
-                    even_hit(k + 2)
-        mm(5, T.eq, T.es, 384, tq, tsc, 240, W, ["eq", kE])
+            odd_block(t + 1, lambda: None)
+            odd_level(0)
+            odd_level(1)
         for b in range(4):
             mm(b, T.eq, T.es, 128 * b, hq, hs, 0, 128, ["eq", kH, kG])
         for b in range(4):
             cp("A", T.ep[:, 256 * b + 128:256 * b + 240], bank(b, 0, K), ["ps%d" % b], ["eg%d" % b])
-        tt(T.mn[:, 0:7], hits(2), T["li%d" % t][:, 0:7], Alu.min,
-           ["do2", "al%d" % t] + ["dE%d" % k for k in range(7)], ["mn"])
+        tt(T.mn[:, 0:7], hits(2), T["li%d" % t][:, 0:7], Alu.min, ["do2", "al%d" % t], ["mn"])
+        if not last:
+            odd_level(2)
         ts(T.oe[:, 0:7], T.mn[:, 0:7], 112.0, None, Alu.add, None, ["mn"], ["oe"])
         cp("A", T.ga[:], T.ep[:, 768:1024].indirect(T.oe[:, 0:7]), ["oe", "eo3", "eg3", "ez3"], ["ga"])
         for b in range(4):
+            if not last and b < 3:
+                odd_level(3 + b)
             out = T.xf[:, b:4 * C:8] if last else T.xs[:, 512 + b:960:4]
             if b == 3:
                 tt(out, T.ga[:], bank(5, 0, K), Alu.add, ["ga", "ps5"], [XE[b]])
                 continue
             tt(out, T.ep[:, 256 * b:256 * b + 256].indirect(T.oe[:, 0:7]), T.vp[:, W * b + 240:W * b + 352], Alu.add,
                ["oe", "eo%d" % b, "eg%d" % b, "ez%d" % b, "vo%d" % b], [XE[b]])
+        if not last:
+            odd_level(6)
 
     quant(T.fq, T.fs, 0, C, T.xf[:], XO + XE, ["fq"])
     mm(4, T.vq, T.vs, 0, T.fq, T.fs, 0, C, ["vq", "fq"])

@@ -2,13 +2,22 @@ from concourse.mybir import dt, AluOpType as Alu, ActivationFunctionType as Act
 
 N, C, K, ROUNDS = 8, 224, 112, 3
 W = 368
+VW = 352
 RW = 337
+CX = C + 1
 CW = 120
-DW = K + 1
+DW = K + 2
 NS = K + 1 + 8 * C
 UNIT = 4096.0
+HIT = 4352.0
 BIG = 3.0e29
-X4, U8, BF, F32, F16 = "float8_e4m3fn_x4", "uint8", "bfloat16", "float32", "float16"
+X4, U8, BF, F32, F16, U16 = "float8_e4m3fn_x4", "uint8", "bfloat16", "float32", "float16", "uint16"
+
+WAVE = """
+O2 - O3 E0 O4 E1 O5 q0 E2 O6 q1 E3 O7 j02 q2 E4 J02 q3 d4 E5 d5 c0 c1 c2 E6 a0 d6 cx j35 q4 E7 a1 d7 J35 q5
+P0 a2 c3 c4 q6 P1 a3 c5 j67 cn q7 P2 a4 J67 n0 n1 P3 c6 c7 n2 a5 a6 a7 P4 k03 n3 P5 K03 n4 P6 D5 dl t1 t2 t3
+P7 D6 v0 v1 v2 v3 k46 m0 m1 m2 m3 n5 y6 K46 n7 n6 y7 t4 t5 t6 t7 m4 m5 m6 m7 two four3 one
+""".split()
 
 SCRATCH = {
     "xin": ("sbuf", [128, 4 * C], BF), "xs": ("sbuf", [128, 1024], BF), "xf": ("sbuf", [128, 4 * C], BF),
@@ -16,26 +25,27 @@ SCRATCH = {
     "wq": ("sbuf", [128, 512], X4), "wp": ("sbuf", [128, 512], U8),
     "un": ("sbuf", [128, 2048], BF), "eq": ("sbuf", [128, 512], X4), "es": ("sbuf", [128, 512], U8),
     "fq": ("sbuf", [128, C], X4), "fs": ("sbuf", [128, C], U8), "yo": ("sbuf", [128, C], F32),
-    "vp": ("sbuf", [128, 4 * W], BF), "ep": ("sbuf", [128, 4 * 256], BF),
+    "vp": ("sbuf", [128, 4 * VW], BF), "ep": ("sbuf", [128, 4 * 256], BF),
     "zt": ("sbuf", [128, 512], BF), "zq": ("sbuf", [128, 128], X4), "zs": ("sbuf", [128, 128], U8),
     "ht": ("sbuf", [128, 512], BF),
-    "sc": ("sbuf", [128, C], F32), "mk": ("sbuf", [128, K], F32), "big": ("sbuf", [128, C], F32),
+    "sc": ("sbuf", [128, C], F32), "mk": ("sbuf", [128, K], F32), "big": ("sbuf", [128, K], F32),
     "rr": ("sbuf", [128, 8 * RW], F32), "cn": ("sbuf", [128, CW], F32),
-    "e1": ("sbuf", [128, 8 * C], BF), "c1": ("sbuf", [128, 8 * C], BF), "s1": ("sbuf", [128, 4 * C], BF),
-    "e2": ("sbuf", [128, 8 * CW], BF), "c2": ("sbuf", [128, 8 * CW], BF), "s2": ("sbuf", [128, 8 * CW], F16),
+    "d1": ("sbuf", [128, 8 * C], BF), "e1": ("sbuf", [128, 8 * C], BF), "c1": ("sbuf", [128, 8 * CX], BF),
+    "s1": ("sbuf", [128, 8 * CX], BF), "one": ("sbuf", [128, C], BF), "tb": ("sbuf", [128, 9], F32),
+    "e2": ("sbuf", [128, 8 * CW + 1], BF), "c2": ("sbuf", [128, 8 * CW + 1], BF), "s2": ("sbuf", [128, 26 * CW], F16),
+    "d2": ("sbuf", [128, 8 * CW], BF),
     "ga": ("sbuf", [128, K], BF),
-    "zer": ("sbuf", [128, 7 * DW], BF), "nj": ("sbuf", [128, 8], BF), "ej": ("sbuf", [128, 8], BF),
-    "mu": ("sbuf", [128, 8], BF), "one": ("sbuf", [128, C], BF),
-    "tb": ("sbuf", [128, 16], F32), "td": ("sbuf", [128, 8], F32), "dl": ("sbuf", [128, CW], F16),
-    "m2": ("sbuf", [128, 32], F32),
-    "mh": ("sbuf", [128, 8], "uint16"), "sl": ("sbuf", [128, NS], BF), "bb": ("sbuf", [128, 128], BF),
-    "tt": ("sbuf", [128, 128], BF), "off": ("sbuf", [128, 8], "uint16"),
-    "idc": ("sbuf", [128, 352], BF), "ll": ("sbuf", [128, K], BF), "idb": ("sbuf", [128, 128], BF),
-    "pi": ("sbuf", [128, 2], "int32"), "pf": ("sbuf", [128, 1], F32), "c22": ("sbuf", [128, 22], F32),
-    "ids": ("sbuf", [128, 22], BF), "nb": ("sbuf", [128, 22], F32),
+    "zer": ("sbuf", [128, 7 * DW], BF), "nj": ("sbuf", [128, 16], BF), "ej": ("sbuf", [128, 16], BF),
+    "nf": ("sbuf", [128, 3], F32), "mu": ("sbuf", [128, 8], BF), "dl": ("sbuf", [128, CW], F16),
+    "mh": ("sbuf", [128, 8], U16), "sl": ("sbuf", [128, NS], BF), "bb": ("sbuf", [128, 128], BF),
+    "tt": ("sbuf", [128, 128], BF),
+    "idc": ("sbuf", [128, VW], BF), "idg": ("sbuf", [128, VW], BF), "idb": ("sbuf", [128, 128], BF),
+    "ll": ("sbuf", [128, K], BF), "lg": ("sbuf", [128, K], BF),
+    "pi": ("sbuf", [128, 2], "int32"), "pf": ("sbuf", [128, 1], F32), "c15": ("sbuf", [128, 15], F32),
+    "ids": ("sbuf", [128, 15], BF), "apart": ("sbuf", [128, 8], BF),
     "dd": ("sbuf", [128, 21 * DW], BF), "do": ("sbuf", [128, 21 * DW], BF), "rm": ("sbuf", [128, 7 * DW], BF),
-    "oo": ("sbuf", [128, 8], "uint16"), "oe": ("sbuf", [128, 8], "uint16"), "mn": ("sbuf", [128, 8], F32),
-    "pls": ("sbuf", [128, 352], F32), "opb": ("sbuf", [128, K], F32),
+    "oo": ("sbuf", [128, 8], U16), "oe": ("sbuf", [128, 8], U16), "mn": ("sbuf", [128, 8], F32),
+    "pls": ("sbuf", [128, VW], F32), "opb": ("sbuf", [128, K], F32),
     "ps": ("psum", [128, 4096], F32),
 }
 for _t in range(ROUNDS):
@@ -43,11 +53,11 @@ for _t in range(ROUNDS):
     SCRATCH["ts%d" % _t] = ("sbuf", [128, W], U8)
     SCRATCH["hq%d" % _t] = ("sbuf", [128, 240], X4)
     SCRATCH["hs%d" % _t] = ("sbuf", [128, 240], U8)
-    SCRATCH["lo%d" % _t] = ("sbuf", [128, 8], F32)
-    SCRATCH["li%d" % _t] = ("sbuf", [128, 8], F32)
+    SCRATCH["lo%d" % _t] = ("sbuf", [128, 8], U16)
+    SCRATCH["li%d" % _t] = ("sbuf", [128, 8], U16)
 
 SEMAPHORES = ["cV", "cA", "cP", "cG", "dx", "dwc", "dws", "dv", "dout", "left"] + \
-    ["a%s%d" % (k, t) for k in "phl" for t in range(ROUNDS)]
+    ["a%s%d" % (k, t) for k in "plh" for t in range(ROUNDS)]
 
 
 def bits(engs):
@@ -60,7 +70,7 @@ def routes(T, topo, t, kind, r):
     q, s, a = ("tq%d" % t, "ts%d" % t, 240) if kind == "p" else ("hq%d" % t, "hs%d" % t, 112)
     codes = (lambda: T[q][:, a:a + K].bitcast(dt.uint8)), (lambda: T[q][:, 0:K].bitcast(dt.uint8))
     plane = (lambda: T[s][:, a:a + K]), (lambda: T[s][:, 0:K])
-    lst = (lambda: T["lo%d" % t][:, 0:7]), (lambda: T["li%d" % t][:, 0:7])
+    lst = (lambda: T["lo%d" % t][:]), (lambda: T["li%d" % t][:])
     if topo.may_write(src, dst) and (t, kind) != (0, "p"):
         e = topo.engines(src, dst)
         if kind == "l":
@@ -71,7 +81,7 @@ def routes(T, topo, t, kind, r):
     far = [c for c in able if topo.die(c) != topo.die(src)][0]
     e = topo.engines(src, near)
     if kind == "l":
-        return dst, [lst + (far, e, topo.engines(far, dst))]
+        return dst, [lst + (near, e, topo.engines(near, dst))]
     return dst, [codes + (near, e, topo.engines(near, dst)), plane + (far, e, topo.engines(far, dst))]
 
 
@@ -83,7 +93,7 @@ def landing(T, topo, t, kind, r):
 def relay_program(g, core, T, topo):
     left = 0
     for t in range(ROUNDS):
-        for kind in "phl":
+        for kind in "plh":
             for r in range(N):
                 dst, pieces = routes(T, topo, t, kind, r)
                 for _, land, via, e1, e2 in pieces:
@@ -144,7 +154,7 @@ def rank_program(g, core, T, topo):
         total["left"] = total.get("left", 0) + sum(len(p[3]) for p in pieces)
 
     for t in range(ROUNDS):
-        for kind in "phl":
+        for kind in "plh":
             s = "a%s%d" % (kind, t)
             total[s] = landing(T, topo, t, kind, rank)
             wrote[s] = (s, total[s])
@@ -189,59 +199,72 @@ def rank_program(g, core, T, topo):
     def quant(q, s, a, b, in_, r, w):
         op("V", lambda: V.quantize_mx(q[:, a:b], s[:, a:b], in_), r, w)
 
-    def level(k, o, n, d0, r, blk, prev):
+    def level(blk, k):
+        o, d0, src, prev = {"O": (0, T.sc[:, 1:C:2], "scO", None), "E": (K, bank(5, 0, K), "ps5", "O"),
+                            "P": (C, bank(4, 0, K), "ps4", "E")}[blk]
         b = k * RW + o
-        d1 = T.big[:, 0:n] if k == 0 else T.rr[:, b - RW:b - RW + n]
-        rd = r + ["big", "r0"] + ["r%s%d" % (x, k - 1) for x in (blk, prev) if x and k]
+        d1 = T.big[:] if k == 0 else T.rr[:, b - RW:b - RW + K]
+        rd = [src, "big", "r0"] + ["r%s%d" % (x, k - 1) for x in (blk, prev) if x and k]
         if prev:
             rd.append("r%s%d" % (prev, k))
-        scan(T.rr[:, b + 1:b + 1 + n], d0, d1, T.rr[:, b:b + 1], Alu.max, Alu.min, rd, ["r%s%d" % (blk, k)])
+        scan(T.rr[:, b + 1:b + 1 + K], d0, d1, T.rr[:, b:b + 1], Alu.max, Alu.min, rd, ["r%s%d" % (blk, k)])
 
-    def equal_runs(col, blk):
-        rd = ["r%s%d" % (blk, k) for k in range(8)]
-        yield tt(T.ej[:, 1:8], T.rr[:, RW + col:8 * RW:RW], T.rr[:, col:7 * RW:RW], Alu.is_equal, rd, ["ej"])
-        yield scan(T.nj[:], T.ej[:], T.mu[:], 0.0, Alu.mult, Alu.add, ["ej", "ej0", "mu"], ["nj"])
+    def best(blk, a, b=None):
+        col = C if blk == "E" else RW - 1
+        return T.rr[:, a * RW + col:(a if b is None else b) * RW + col + 1:RW]
 
-    def differ(e, seg):
-        c = seg if seg < 14 else seg + 1
-        out = T.dd[:, seg * DW:seg * DW + K]
-        if e == "V":
-            ts(out, T.ll[:], T.ids[:, c:c + 1], 512.0, Alu.not_equal, Alu.mult, ["ll", "ids"], ["dd%d" % seg])
-        else:
-            op("A", lambda: A.activation(out, T.ll[:], Act.Abs, bias=T.nb[:, c:c + 1], scale=512.0),
-               ["ll", "nb"], ["dd%d" % seg])
+    def same(blk, a, b):
+        o, a = (0 if blk == "E" else 8), max(a, 1)
+        tt(T.ej[:, o + a:o + b + 1], best(blk, a, b), best(blk, a - 1, b - 1), Alu.is_equal,
+           ["r%s%d" % (blk, k) for k in range(a - 1, b + 1)], ["ej%s%d" % (blk, b)])
+
+    def number(blk, a, b):
+        o = 0 if blk == "E" else 8
+        scan(T.nj[:, o + a:o + b + 1], T.ej[:, o + a:o + b + 1], T.mu[:, a:b + 1], T.nj[:, o + a - 1:o + a] if a else 0.0,
+             Alu.mult, Alu.add, ["ej%s%d" % (blk, b), "ej0", "mu"] + ["nj%s%d" % (blk, a - 1)] * (a > 0),
+             ["nj%s%d" % (blk, k) for k in range(a, b + 1)])
+
+    def differ(seg):
+        c = seg if seg < 7 else 8 + seg % 7
+        lst, key = (T.ll, "ll") if seg < 14 else (T.lg, "lg")
+        ts(T.dd[:, seg * DW:seg * DW + K], lst[:], T.ids[:, c:c + 1], 512.0, Alu.not_equal, Alu.mult, [key, "ids"],
+           ["dd%d" % seg])
 
     def first_hit(blk):
         a, b = 7 * blk * DW, 7 * (blk + 1) * DW
         scan(T.do[:, a:b], T.dd[:, a:b], T.rm[:], 4096.0, Alu.min, Alu.add,
-             ["dd%d" % s for s in range(7 * blk, 7 * blk + 7)] + ["ddr", "rm"], ["do%d" % blk])
+             ["dd%d" % s for s in range(7 * blk, 7 * blk + 7)] + ["ddr", "ddx", "rm"], ["do%d" % blk])
 
-    def hits(blk):
-        return T.do[:, 7 * blk * DW + K - 1:7 * (blk + 1) * DW:DW]
+    def hits(blk, x=0):
+        return T.do[:, 7 * blk * DW + K - 1 + x:7 * (blk + 1) * DW:DW]
 
     op("S", lambda: g.sync.dma_start(T.xin[:], T.x[:]), [], ["xin"], "dx")
     iota(T.idb[:], [[1, 128]], 0, -1, ["idb"])
     iota(T.pi[:, 0:1], [[1, 1]], 0, 1, ["pi0"], True)
-    iota(T.c22[:], [[16, 22]], -176, 0, ["c22"])
+    iota(T.c15[:], [[16, 15]], 112 - 176, 0, ["c15"])
+    iota(T.apart[:], [[-C, 8]], 7 * C, 0, ["apart"])
     fill(T.zer[:], 0.0, ["zer"])
     fill(T.xs[:, 448:512], 0.0, ["xpO"])
     fill(T.xs[:, 960:1024], 0.0, ["xpE"])
     fill(T.un[:], 0.0, ["un"])
     afill(T.rr[:, 0:8 * RW:RW], 8, -BIG, ["r0"])
-    afill(T.big[:], C, BIG, ["big"])
+    afill(T.big[:], K, BIG, ["big"])
     afill(T.one[:], C, 1.0, ["one"])
     afill(T.mu[:], 8, -UNIT, ["mu"])
-    afill(T.ej[:, 0:1], 1, 0.0, ["ej0"])
-    afill(T.tb[:, 8:9], 1, float(C), ["tbc"])
-    afill(T.dd[:, K:21 * DW:DW], 21, 512.0, ["ddr"])
+    afill(T.ej[:, 0:16:8], 2, 0.0, ["ej0"])
+    afill(T.tb[:, 8:9], 1, 0.0, ["tb8"])
+    afill(T.e2[:, 7 * CW:7 * CW + 1], 1, -UNIT, ["e2x"])
+    afill(T.dd[:, K:21 * DW:DW], 21, 512.0, ["ddx"])
+    afill(T.dd[:, K + 1:21 * DW:DW], 21, 512.0, ["ddr"])
     afill(T.rm[:], 7 * DW, -1.0, ["rm"])
     fill(T.zt[:, 448:512], 0.0, ["zp"])
     fill(T.ht[:, 448:512], 0.0, ["hp"])
-    fill(T.dl[:, 8:CW], 1.0, ["dlc"])
     for b in range(4):
         ts(T.un[:, 512 * b + b:512 * b + 512:4], T.idb[:], 0.0, None, Alu.is_equal, None, ["idb", "un"], ["un%d" % b])
     op("A", lambda: A.activation(T.mk[:], T.un[:, 0:4 * K:4], Act.Copy, scale=-1.0e29), ["un0"], ["mk"])
-    afill(T.rm[:, K:7 * DW:DW], 7, 4096.0, ["rm"])
+    afill(T.rm[:, K:7 * DW:DW], 7, 128.0, ["rm"])
+    cp("A", T.c1[:, C:8 * CX:CX], T.apart[:], ["apart"], ["c1x"])
+    afill(T.rm[:, K + 1:7 * DW:DW], 7, 4096.0, ["rm"])
 
     XO, XE = ["xO%d" % b for b in range(4)], ["xE%d" % b for b in range(4)]
     for b in range(4):
@@ -249,213 +272,230 @@ def rank_program(g, core, T, topo):
     for b in range(4):
         cp("V", T.xs[:, b:448:4], T.xin[:, 4 + b:4 * C:8], ["xin"], [XO[b]])
 
-    def odd_block(t, between):
+    def odd_scores(t):
         tq, tsc = T["tq%d" % t], T["ts%d" % t]
         quant(tq, tsc, 112, 240, T.xs[:, 0:512], XO + ["xpO"], ["tO%d" % t])
         mm(4, tq, tsc, 112, tq, tsc, 112, 240, ["tO%d" % t])
-        between()
-        tt(T.sc[:, 1:C:2], bank(4, 0, K), T.mk[:], Alu.add, ["ps4", "mk"], ["scO"])
 
-    def odd_level(k):
-        level(k, 0, K, T.sc[:, 1:C:2], ["scO"], "O", None)
+    def odd_mask():
+        tt(T.sc[:, 1:C:2], bank(4, 0, K), T.mk[:], Alu.add, ["ps4", "mk"], ["scO"])
 
     for t in range(ROUNDS):
         last = t == ROUNDS - 1
         tq, tsc, hq, hs = T["tq%d" % t], T["ts%d" % t], T["hq%d" % t], T["hs%d" % t]
+        off, kL = T["lo%d" % t], "lo%d" % t
         kO, kE, kP, kH, kG = "tO%d" % t, "tE%d" % t, "ap%d" % t, "hH%d" % t, "ah%d" % t
         quant(tq, tsc, 240, W, T.xs[:, 512:1024], XE + ["xpE"], [kE])
         send(t, "p", [kE])
         if t == 0:
-            odd_block(0, lambda: quant(T.eq, T.es, 0, 512, T.un[:], ["un%d" % b for b in range(4)], ["eq"]))
+            odd_scores(0)
+            ts(T.pi[:, 1:2], T.pi[:, 0:1], 15, None, Alu.bitwise_and, None, ["pi0"], ["pi1"])
+            quant(T.eq, T.es, 0, 512, T.un[:], ["un%d" % b for b in range(4)], ["eq"])
+            odd_mask()
+            cp("V", T.pf[:], T.pi[:, 1:2], ["pi1"], ["pf"])
+            for b in range(4):
+                fill(T.ep[:, 256 * b + 240:256 * b + 256], 0.0, ["ez%d" % b])
+            level("O", 0)
+            ts(T.dl[:, 8:CW], T.zer[:, 0:K], 1.0, None, Alu.add, None, ["zer"], ["dlc"])
+            ts(T.ids[:], T.c15[:], T.pf[:], None, Alu.add, None, ["c15", "pf"], ["ids"])
+            level("O", 1)
             iota(T.sl[:, 0:K + 1], [[-1, K + 1]], K - 176, 0, ["sl0"])
             iota(T.sl[:, K + 1:NS], [[0, 8], [-1, K], [128, 2]], 223 - 176, 0, ["sl1"])
-            iota(T.idc[:], [[1, 352]], -176, 0, ["idc"])
-        else:
-            mm(5, tq, tsc, 112, tq, tsc, 240, W, [kO, kE])
-            odd_level(7)
+            iota(T.idc[:], [[1, VW]], -176, 0, ["idc"])
+            iota(T.idg[:, 0:K], [[1, K]], 240 - 176, 0, ["idg0"])
+            afill(T.idg[:, K:VW], VW - K, -200.0, ["idg1"])
         if t == 1:
             iota(T.pls[:, 0:112], [[1, K]], C, 0, ["pl0"])
             iota(T.pls[:, 112:240], [[2, 128]], 1, 0, ["pl1"])
-            iota(T.pls[:, 240:352], [[2, K]], 0, 0, ["pl2"])
-            quant(T.vq, T.vs, 0, 128, T.vin[:], ["vin"], ["vq"])
+            iota(T.pls[:, 240:VW], [[2, K]], 0, 0, ["pl2"])
+        mm(5, tq, tsc, 112, tq, tsc, 240, W, [kO, kE])
         mm(6, tq, tsc, 112, tq, tsc, 240, W, [kO, kE])
-        for b in range(4):
-            mm(b, T.eq, T.es, 128 * b, tq, tsc, 112, W, ["eq", kO, kE])
         cp("A", T.sc[:, 0:C:2], bank(6, 0, K), ["ps6"], ["scE"])
-        for b in range(4):
-            cp("A", T.vp[:, W * b + 112:W * b + 352], bank(b, 0, 240), ["ps%d" % b], ["vo%d" % b])
-        if t == 0:
-            ts(T.pi[:, 1:2], T.pi[:, 0:1], 15, None, Alu.bitwise_and, None, ["pi0"], ["pi1"])
-            for b in range(4):
-                fill(T.ep[:, 256 * b + 240:256 * b + 256], 0.0, ["ez%d" % b])
-            cp("V", T.pf[:], T.pi[:, 1:2], ["pi1"], ["pf"])
+        apart = set()
 
-        def own_level(k):
+        def aside():
+            if t == 1:
+                quant(T.vq, T.vs, 0, 128, T.vin[:], ["vin"], ["vq"])
+
+        def loads():
             if t == 0:
-                level(k, 0, C, T.sc[:], ["scO", "scE"], "E", None)
-            else:
-                level(k, K, K, bank(5, 0, K), ["ps5"], "E", "O")
+                op("S", lambda: g.sync.dma_start(T.wq[:].bitcast(dt.uint8), T.wc[:]), ["rE6"], ["wq"], "dwc")
+                op("S", lambda: g.sync.dma_start(T.wp[:], T.ws[:]), [], ["wp"], "dws")
+                op("S", lambda: g.sync.dma_start(T.vin[:], T.v[:]), [], ["vin"], "dv")
+
+        def distance(k):
+            apart.add(k)
+            op("A", lambda: A.activation(T.d1[:, k * C:(k + 1) * C], T.sc[:], Act.Identity, bias=best("E", k),
+                                         scale=-1.0), ["scO", "scE", "rE%d" % k], ["d1%d" % k])
 
         def own_equal(k):
-            ts(T.e1[:, k * C:(k + 1) * C], T.sc[:], T.rr[:, k * RW + C:k * RW + C + 1], UNIT, Alu.is_equal, Alu.mult,
-               ["scO", "scE", "rE%d" % k], ["e1%d" % k])
+            out = T.e1[:, k * C:(k + 1) * C]
+            if k in apart:
+                ts(out, T.d1[:, k * C:(k + 1) * C], 0.0, HIT, Alu.is_equal, Alu.mult, ["d1%d" % k], ["e1%d" % k])
+            else:
+                ts(out, T.sc[:], best("E", k), HIT, Alu.is_equal, Alu.mult, ["scO", "scE", "rE%d" % k], ["e1%d" % k])
 
         def own_count(k):
-            seg = T.c1[:, k * C:(k + 1) * C]
-            scan(seg, T.e1[:, k * C:(k + 1) * C], T.zer[:, 0:C], T.nj[:, k:k + 1], Alu.add, Alu.min,
-                 ["e1%d" % k, "zer", "nj"], ["c1%d" % k])
-            if k < 4:
-                op("A", lambda: A.activation(seg, seg, Act.Relu, bias=1.0, accum_out=T.tb[:, k:k + 1]),
-                   ["c1%d" % k], ["tb%d" % k, "c1%d" % k])
+            scan(T.c1[:, k * CX:k * CX + C], T.e1[:, k * C:(k + 1) * C], T.one[:], T.nj[:, k:k + 1], Alu.add, Alu.min,
+                 ["e1%d" % k, "one", "njE%d" % k], ["c1%d" % k])
 
         def own_name(k):
-            scan(T.s1[:, (k - 4) * C:(k - 3) * C], T.c1[:, k * C:(k + 1) * C], T.one[:], -8 * UNIT, Alu.max, Alu.add,
-                 ["c1%d" % k, "one"], ["s1%d" % k])
+            op("A", lambda: A.activation(T.s1[:, k * CX:(k + 1) * CX], T.c1[:, k * CX:(k + 1) * CX], Act.Relu,
+                                         accum_out=T.tb[:, k:k + 1]), ["c1%d" % k, "c1x"], ["tb%d" % k, "s1%d" % k])
 
-        own_level(0)
-        if t == 0:
-            ts(T.ids[:], T.c22[:], T.pf[:], None, Alu.add, None, ["c22", "pf"], ["ids"])
-            ts(T.nb[:], T.c22[:], T.pf[:], -512.0, Alu.add, Alu.mult, ["c22", "pf"], ["nb"])
-        own_level(1)
-        for k in range(2, 8):
-            own_equal(k - 2)
-            own_level(k)
-        runs = equal_runs(C, "E")
-        own_equal(6)
-        next(runs)
-        own_equal(7)
-        next(runs)
-        cp("V", T.cn[:, 0:8], T.rr[:, C:8 * RW:RW], ["rE%d" % k for k in range(8)], ["cn0"])
-        if t == 0:
-            op("S", lambda: g.sync.dma_start(T.wq[:].bitcast(dt.uint8), T.wc[:]), ["e17"], ["wq"], "dwc")
-            op("S", lambda: g.sync.dma_start(T.wp[:], T.ws[:]), [], ["wp"], "dws")
-            op("S", lambda: g.sync.dma_start(T.vin[:], T.v[:]), [], ["vin"], "dv")
-        for k in range(5):
-            own_count(k)
-
-        mm(4, tq, tsc, 112, tq, tsc, 0, 128, [kO, kP])
-        mm(7, tq, tsc, 112, tq, tsc, 0, 128, [kO, kP])
-        for b in range(4):
-            mm(b, T.eq, T.es, 128 * b, tq, tsc, 0, 128, ["eq", kO, kP])
-        cp("A", T.cn[:, 8:CW], bank(7, 0, K), ["ps7"], ["cn1"])
-        for b in range(4):
-            cp("A", T.vp[:, W * b:W * b + K], bank(b, 0, K), ["ps%d" % b], ["vP%d" % b])
-
-        def new_equal(k):
-            best = T.rr[:, k * RW + RW - 1:k * RW + RW]
+        def partner_level(k):
             if k == 0:
-                ts(T.c2[:, 0:CW], T.cn[:], best, -UNIT, Alu.not_equal, Alu.mult, ["cn0", "cn1", "rP0"], ["c20"])
-            else:
-                ts(T.e2[:, k * CW:(k + 1) * CW], T.cn[:], best, UNIT, Alu.is_equal, Alu.mult,
-                   ["cn0", "cn1", "rP%d" % k], ["e2%d" % k])
+                mm(4, tq, tsc, 112, tq, tsc, 0, 128, [kO, kP])
+                mm(7, tq, tsc, 112, tq, tsc, 0, 128, [kO, kP])
+                for b in range(4):
+                    mm(b, T.eq, T.es, 128 * b, tq, tsc, 0, VW, ["eq", kO, kE, kP])
+            level("P", k)
+            if k == 0:
+                cp("A", T.cn[:, 8:CW], bank(7, 0, K), ["ps7"], ["cn1"])
 
-        def count(k):
-            scan(T.c2[:, k * CW:(k + 1) * CW], T.e2[:, k * CW:(k + 1) * CW], T.zer[:, 0:CW], T.nj[:, k:k + 1],
-                 Alu.add, Alu.min, ["e2%d" % k, "zer", "nj"], ["c2%d" % k])
-
-        def name(k):
-            n = 4 * (k % 2) + k // 2
-            scan(T.s2[:, n * CW:(n + 1) * CW], T.c2[:, k * CW:(k + 1) * CW], T.dl[:], -8 * UNIT, Alu.max, Alu.add,
-                 ["c2%d" % k, "dl", "dlc"], ["s2%d" % k])
-
-        def own_tail():
-            cp("V", T.tb[:, 4:8], T.s1[:, C - 1:4 * C:C], ["s14", "s15", "s16", "s17"], ["tb4"])
+        def own_values():
+            cp("V", T.cn[:, 0:8], best("E", 0, 7), ["rE%d" % k for k in range(8)], ["cn0"])
 
         def steps():
-            tt(T.td[:], T.tb[:, 0:8], T.tb[:, 1:9], Alu.subtract, ["tbc"] + ["tb%d" % k for k in range(5)], ["td"])
+            tt(T.dl[:, 0:8], T.tb[:, 0:8], T.tb[:, 1:9], Alu.subtract, ["tb%d" % k for k in range(9)], ["dl"])
 
-        def steps_on():
-            ts(T.dl[:, 0:8], T.td[:], float(C), None, Alu.add, None, ["td"], ["dl"])
+        def values(b):
+            cp("A", T.vp[:, VW * b:VW * (b + 1)], bank(b, 0, VW), ["ps%d" % b], ["vp%d" % b])
 
-        runs = equal_runs(RW - 1, "P")
-        between = [[(own_count, 5), (own_count, 6)], [(own_count, 7), (own_name, 4)], [(own_name, 5), (own_name, 6)],
-                   [(own_name, 7), (new_equal, 0)], [(new_equal, 1), (own_tail,), (new_equal, 2)],
-                   [(new_equal, 3), (steps,)], [(new_equal, 4), (steps_on,)],
-                   [(new_equal, 5), (new_equal, 6), (next, runs), (name, 0), (new_equal, 7), (next, runs)]]
-        for k in range(8):
-            level(k, C, K, bank(4, 0, K), ["ps4"], "P", "E")
-            for call in between[k]:
-                call[0](*call[1:])
-        for k in range(1, 8):
-            count(k)
-        for k in range(1, 8):
-            name(k)
-        for a in range(4):
-            cp("V", T.m2[0:32, 8 * a:8 * a + 8], T.s2[32 * a:32 * a + 32, CW - 1:8 * CW:CW],
-               ["s2%d" % k for k in range(8)], ["m2%d" % a])
-        for h in range(4):
-            cp("V", T.mh[32 * h:32 * h + 32, :], T.m2[0:32, h:32:4], ["m20", "m21", "m22", "m23"], ["mh%d" % h])
-        cp("V", T.bb[:], T.sl[:].indirect(T.mh[:]), ["mh0", "mh1", "mh2", "mh3", "sl0", "sl1"], ["bb"])
+        def far(k):
+            apart.add(8 + k)
+            op("A", lambda: A.activation(T.d2[:, k * CW:(k + 1) * CW], T.cn[:], Act.Identity, bias=best("P", k),
+                                         scale=-1.0), ["cn0", "cn1", "rP%d" % k], ["d2%d" % k])
+
+        def seg(buf, k):
+            return buf[:, k * CW + k // 7:(k + 1) * CW + k // 7]
+
+        def slot(k):
+            return 3 * (k % 2) + k // 2 if k < 6 else 18 + k
+
+        def equal(k):
+            if k == 0:
+                ts(seg(T.c2, 0), T.cn[:], best("P", 0), -UNIT, Alu.not_equal, Alu.mult, ["cn0", "cn1", "rP0"], ["c20"])
+            elif 8 + k in apart:
+                ts(seg(T.e2, k), T.d2[:, k * CW:(k + 1) * CW], 0.0, UNIT, Alu.is_equal, Alu.mult, ["d2%d" % k],
+                   ["e2%d" % k])
+            else:
+                ts(seg(T.e2, k), T.cn[:], best("P", k), UNIT, Alu.is_equal, Alu.mult, ["cn0", "cn1", "rP%d" % k],
+                   ["e2%d" % k])
+
+        def last_number():
+            ts(T.nj[:, 15:16], best("P", 7), best("P", 6), T.nf[:, 2:3], Alu.is_equal, Alu.mult,
+               ["rP6", "rP7", "nf"], ["njP7"])
+
+        def wide_numbers():
+            scan(T.nf[:], T.ej[:, 12:15], T.mu[:, 0:3], T.nj[:, 11:12], Alu.mult, Alu.add, ["ejP6", "mu", "njP3"], ["nf"])
+
+        def count(k):
+            a, b = k * CW, (k + 1) * CW + k // 7
+            scan(T.c2[:, a:b], T.e2[:, a:b], T.zer[:, 0:b - a], T.nj[:, 8 + k:9 + k], Alu.add, Alu.min,
+                 ["e2%d" % k, "e2x", "zer", "njP%d" % k], ["c2%d" % k])
+
+        def name(k):
+            scan(T.s2[:, slot(k) * CW:(slot(k) + 1) * CW], seg(T.c2, k), T.dl[:], -8 * UNIT, Alu.max, Alu.add,
+                 ["c2%d" % k, "dl", "dlc"], ["s2%d" % k])
+
+        def gather_names():
+            for a in range(1, 4):
+                cp("V", T.s2[0:32, (6 * a + 1) * CW - 1:6 * (a + 1) * CW:CW], T.s2[32 * a:32 * a + 32, CW - 1:6 * CW:CW],
+                   ["s2%d" % k for k in range(6)], ["m2%d" % a])
+
+        def deal_names():
+            for h in range(3):
+                cp("V", T.mh[32 * h:32 * h + 32, :], T.s2[0:32, (h + 1) * CW - 1:24 * CW:3 * CW],
+                   ["s2%d" % k for k in range(6)] + ["m21", "m22", "m23"], ["mh%d" % h])
+
+        def move_names(h):
+            for a in range(4):
+                cp("V", T.mh[32 * h:32 * h + 32, 2 * a:2 * a + 2],
+                   T.s2[32 * a:32 * a + 32, (slot(2 * h) + 1) * CW - 1:(slot(2 * h) + 2) * CW:CW],
+                   ["s2%d" % (2 * h), "s2%d" % (2 * h + 1)], ["mh%d%d" % (h, a)])
+
+        words = {"-": aside, "cx": loads, "cn": own_values, "dl": steps, "y7": last_number, "y6": wide_numbers, "two": gather_names,
+                 "one": deal_names, "four2": lambda: move_names(2), "four3": lambda: move_names(3)}
+        calls = {"O": lambda k: level("O", k), "E": lambda k: level("E", k), "P": partner_level, "d": distance,
+                 "q": own_equal, "c": own_count, "a": own_name, "D": far, "v": values, "n": equal, "t": count, "m": name,
+                 "j": lambda a, b: same("E", a, b), "J": lambda a, b: number("E", a, b),
+                 "k": lambda a, b: same("P", a, b), "K": lambda a, b: number("P", a, b)}
+        wave = WAVE
+        if t == 0:
+            wave = sorted(WAVE, key=lambda x: x[0] not in "OE-qcajJd" or x in ("dl", "c6", "c7", "a6", "a7"))
+        for word in wave:
+            if word in words:
+                words[word]()
+            else:
+                calls[word[0]](*[int(x) for x in word[1:]])
+
+        cp("V", T.bb[:], T.sl[:].indirect(T.mh[:]),
+           ["mh0", "mh1", "mh2", "sl0", "sl1"] + ["mh3%d" % a for a in range(4)], ["bb"])
         op("V", lambda: V.transpose(T.tt[:], T.bb[:]), ["bb"], ["tt"])
-        ts(T.off[:], T.tt[:, 0:128:16], 176.0, None, Alu.add, None, ["tt"], ["off"])
+        ts(off[:], T.tt[:, 0:128:16], 176.0, None, Alu.add, None, ["tt"], [kL])
+        send(t, "l", [kL])
         for b in (0, 2, 1, 3):
-            cp("VVAA"[b], T.zt[:, b:448:4], T.vp[:, W * b:W * b + 352].indirect(T.off[:, 0:7]),
-               ["off", "vo%d" % b, "vP%d" % b], ["z%d" % b])
-        cp("V", T.ll[:], T.idc[:].indirect(T.off[:, 0:7]), ["off", "idc"], ["ll"])
+            cp("VVAA"[b], T.zt[:, b:448:4], T.vp[:, VW * b:VW * (b + 1)].indirect(off[:, 0:7]), [kL, "vp%d" % b],
+               ["z%d" % b])
+        cp("V", T.ll[:], T.idc[:].indirect(off[:, 0:7]), [kL, "idc"], ["ll"])
         quant(T.zq, T.zs, 0, 128, T.zt[:], ["z0", "z1", "z2", "z3", "zp"], ["zq"])
         for b in (0, 2, 1, 3):
             mm(4 + b, T.wq, T.wp, 128 * b, T.zq, T.zs, 0, 128, ["wq", "wp", "zq"])
-        for s in range(7):
-            differ("V", s)
-        for s in range(7, 9):
-            differ("A", s)
+        for s in range(10):
+            differ(s)
         for b in (0, 2, 1, 3):
             if b < 2:
                 ts(T.ht[:, b:448:4], bank(4 + b, 0, K), 0.03125, None, Alu.mult, None, ["ps%d" % (4 + b)], ["h%d" % b])
             else:
                 op("A", lambda: A.activation(T.ht[:, b:448:4], bank(4 + b, 0, K), Act.Copy, scale=0.03125),
                    ["ps%d" % (4 + b)], ["h%d" % b])
-        first_hit(0)
+        for s in range(10, 14):
+            differ(s)
         quant(hq, hs, 112, 240, T.ht[:], ["h0", "h1", "h2", "h3", "hp"], [kH])
         send(t, "h", [kH])
         for b in range(4):
             mm(b, T.eq, T.es, 128 * b, hq, hs, 112, 240, ["eq", kH])
-        ts(T["lo%d" % t][:, 0:7], hits(0), 0.0, 128.0, Alu.min, Alu.add, ["do0"], ["lo%d" % t])
-        send(t, "l", ["lo%d" % t])
-        for s in range(9, 12):
-            differ("A", s)
-        for s in (12, 13, 14, 15, 16, 17):
-            differ("V", s)
+        mm(5, T.eq, T.es, 384, tq, tsc, 240, W, ["eq", kE])
+        cp("A", T.lg[:], T.idg[:].indirect(T["li%d" % t][:, 0:7]), ["al%d" % t, "idg0", "idg1"], ["lg"])
         for b in range(4):
             cp("A", T.ep[:, 256 * b:256 * b + 128], bank(b, 0, 128), ["ps%d" % b], ["eo%d" % b])
+        first_hit(0)
         first_hit(1)
-        for s in (18, 19, 20):
-            differ("V", s)
-        ts(T.oo[:, 0:7], hits(1), 0.0, 112.0, Alu.min, Alu.add, ["do1"], ["oo"])
-        first_hit(2)
+        ts(T.oo[:, 0:7], hits(0), 0.0, 112.0, Alu.min, Alu.add, ["do0"], ["oo"])
+        for s in range(14, 21):
+            differ(s)
         for b in range(4):
             out = T.xf[:, 4 + b:4 * C:8] if last else T.xs[:, b:448:4]
-            tt(out, T.ep[:, 256 * b:256 * b + 128].indirect(T.oo[:, 0:7]), T.vp[:, W * b + 112:W * b + 224], Alu.add,
-               ["oo", "eo%d" % b, "vo%d" % b], [XO[b]])
-        mm(5, T.eq, T.es, 384, tq, tsc, 240, W, ["eq", kE])
+            tt(out, T.ep[:, 256 * b:256 * b + 128].indirect(T.oo[:, 0:7]), T.vp[:, VW * b + 112:VW * b + 224], Alu.add,
+               ["oo", "eo%d" % b, "vp%d" % b], [XO[b]])
+        first_hit(2)
         if last:
-            cp("A", T.opb[:], T.pls[:].indirect(T.off[:, 0:7]), ["off", "pl0", "pl1", "pl2"], ["opb"])
+            cp("A", T.opb[:], T.pls[:].indirect(off[:, 0:7]), [kL, "pl0", "pl1", "pl2"], ["opb"])
             for k in range(8):
                 op("S", lambda: g.sync.dma_start(T.op[k:k + 1, :], T.opb[16 * k:16 * k + 1, :]), ["opb"], [], "dout")
         else:
-            odd_block(t + 1, lambda: None)
-            odd_level(0)
-            odd_level(1)
-        for b in range(4):
-            mm(b, T.eq, T.es, 128 * b, hq, hs, 0, 128, ["eq", kH, kG])
-        for b in range(4):
-            cp("A", T.ep[:, 256 * b + 128:256 * b + 240], bank(b, 0, K), ["ps%d" % b], ["eg%d" % b])
-        tt(T.mn[:, 0:7], hits(2), T["li%d" % t][:, 0:7], Alu.min, ["do2", "al%d" % t], ["mn"])
+            odd_scores(t + 1)
+        tt(T.mn[:, 0:7], hits(1), hits(2, 1), Alu.min, ["do1", "do2"], ["mn"])
+        ts(T.oe[:, 0:7], T.mn[:, 0:7], 128.0, 112.0, Alu.min, Alu.add, ["mn"], ["oe"])
         if not last:
-            odd_level(2)
-        ts(T.oe[:, 0:7], T.mn[:, 0:7], 112.0, None, Alu.add, None, ["mn"], ["oe"])
+            odd_mask()
+        for b in (0, 3, 1, 2):
+            mm(b, T.eq, T.es, 128 * b, hq, hs, 0, 128, ["eq", kH, kG])
+        for b in (0, 3, 1, 2):
+            cp("AVAA"[b], T.ep[:, 256 * b + 128:256 * b + 240], bank(b, 0, K), ["ps%d" % b], ["eg%d" % b])
         cp("A", T.ga[:], T.ep[:, 768:1024].indirect(T.oe[:, 0:7]), ["oe", "eo3", "eg3", "ez3"], ["ga"])
         for b in range(4):
-            if not last and b < 3:
-                odd_level(3 + b)
             out = T.xf[:, b:4 * C:8] if last else T.xs[:, 512 + b:960:4]
             if b == 3:
                 tt(out, T.ga[:], bank(5, 0, K), Alu.add, ["ga", "ps5"], [XE[b]])
                 continue
-            tt(out, T.ep[:, 256 * b:256 * b + 256].indirect(T.oe[:, 0:7]), T.vp[:, W * b + 240:W * b + 352], Alu.add,
-               ["oe", "eo%d" % b, "eg%d" % b, "ez%d" % b, "vo%d" % b], [XE[b]])
+            tt(out, T.ep[:, 256 * b:256 * b + 256].indirect(T.oe[:, 0:7]), T.vp[:, VW * b + 240:VW * b + 352], Alu.add,
+               ["oe", "eo%d" % b, "eg%d" % b, "ez%d" % b, "vp%d" % b], [XE[b]])
+            if b == 0 and not last:
+                level("O", 0)
         if not last:
-            odd_level(6)
+            level("O", 1)
 
     quant(T.fq, T.fs, 0, C, T.xf[:], XO + XE, ["fq"])
     mm(4, T.vq, T.vs, 0, T.fq, T.fs, 0, C, ["vq", "fq"])

from concourse.mybir import dt, AluOpType as Alu, ActivationFunctionType as Act

N, C, K, ROUNDS = 8, 224, 112, 3
W = 368
VW = 352
RW = 337
CX = C + 1
CW = 120
DW = K + 2
NS = K + 1 + 8 * C
UNIT = 4096.0
HIT = 4352.0
BIG = 3.0e29
X4, U8, BF, F32, F16, U16 = "float8_e4m3fn_x4", "uint8", "bfloat16", "float32", "float16", "uint16"

WAVE = """
O2 - O3 E0 O4 E1 O5 q0 E2 O6 q1 E3 O7 j02 q2 E4 J02 q3 d4 E5 d5 c0 c1 c2 E6 a0 d6 cx j35 q4 E7 a1 d7 J35 q5
P0 a2 c3 c4 q6 P1 a3 c5 j67 cn q7 P2 a4 J67 n0 n1 P3 c6 c7 n2 a5 a6 a7 P4 k03 n3 P5 K03 n4 P6 D5 dl t1 t2 t3
P7 D6 v0 v1 v2 v3 k46 m0 m1 m2 m3 n5 y6 K46 n7 n6 y7 t4 t5 t6 t7 m4 m5 m6 m7 two four3 one
""".split()

SCRATCH = {
    "xin": ("sbuf", [128, 4 * C], BF), "xs": ("sbuf", [128, 1024], BF), "xf": ("sbuf", [128, 4 * C], BF),
    "vin": ("sbuf", [128, 512], BF), "vq": ("sbuf", [128, 128], X4), "vs": ("sbuf", [128, 128], U8),
    "wq": ("sbuf", [128, 512], X4), "wp": ("sbuf", [128, 512], U8),
    "un": ("sbuf", [128, 2048], BF), "eq": ("sbuf", [128, 512], X4), "es": ("sbuf", [128, 512], U8),
    "fq": ("sbuf", [128, C], X4), "fs": ("sbuf", [128, C], U8), "yo": ("sbuf", [128, C], F32),
    "vp": ("sbuf", [128, 4 * VW], BF), "ep": ("sbuf", [128, 4 * 256], BF),
    "zt": ("sbuf", [128, 512], BF), "zq": ("sbuf", [128, 128], X4), "zs": ("sbuf", [128, 128], U8),
    "ht": ("sbuf", [128, 512], BF),
    "sc": ("sbuf", [128, C], F32), "mk": ("sbuf", [128, K], F32), "big": ("sbuf", [128, K], F32),
    "rr": ("sbuf", [128, 8 * RW], F32), "cn": ("sbuf", [128, CW], F32),
    "d1": ("sbuf", [128, 8 * C], BF), "e1": ("sbuf", [128, 8 * C], BF), "c1": ("sbuf", [128, 8 * CX], BF),
    "s1": ("sbuf", [128, 8 * CX], BF), "one": ("sbuf", [128, C], BF), "tb": ("sbuf", [128, 9], F32),
    "e2": ("sbuf", [128, 8 * CW + 1], BF), "c2": ("sbuf", [128, 8 * CW + 1], BF), "s2": ("sbuf", [128, 26 * CW], F16),
    "d2": ("sbuf", [128, 8 * CW], BF),
    "ga": ("sbuf", [128, K], BF),
    "zer": ("sbuf", [128, 7 * DW], BF), "nj": ("sbuf", [128, 16], BF), "ej": ("sbuf", [128, 16], BF),
    "nf": ("sbuf", [128, 3], F32), "mu": ("sbuf", [128, 8], BF), "dl": ("sbuf", [128, CW], F16),
    "mh": ("sbuf", [128, 8], U16), "sl": ("sbuf", [128, NS], BF), "bb": ("sbuf", [128, 128], BF),
    "tt": ("sbuf", [128, 128], BF),
    "idc": ("sbuf", [128, VW], BF), "idg": ("sbuf", [128, VW], BF), "idb": ("sbuf", [128, 128], BF),
    "ll": ("sbuf", [128, K], BF), "lg": ("sbuf", [128, K], BF),
    "pi": ("sbuf", [128, 2], "int32"), "pf": ("sbuf", [128, 1], F32), "c15": ("sbuf", [128, 15], F32),
    "ids": ("sbuf", [128, 15], BF), "apart": ("sbuf", [128, 8], BF),
    "dd": ("sbuf", [128, 21 * DW], BF), "do": ("sbuf", [128, 21 * DW], BF), "rm": ("sbuf", [128, 7 * DW], BF),
    "oo": ("sbuf", [128, 8], U16), "oe": ("sbuf", [128, 8], U16), "mn": ("sbuf", [128, 8], F32),
    "pls": ("sbuf", [128, VW], F32), "opb": ("sbuf", [128, K], F32),
    "ps": ("psum", [128, 4096], F32),
}
for _t in range(ROUNDS):
    SCRATCH["tq%d" % _t] = ("sbuf", [128, W], X4)
    SCRATCH["ts%d" % _t] = ("sbuf", [128, W], U8)
    SCRATCH["hq%d" % _t] = ("sbuf", [128, 240], X4)
    SCRATCH["hs%d" % _t] = ("sbuf", [128, 240], U8)
    SCRATCH["lo%d" % _t] = ("sbuf", [128, 8], U16)
    SCRATCH["li%d" % _t] = ("sbuf", [128, 8], U16)

SEMAPHORES = ["cV", "cA", "cP", "cG", "dx", "dwc", "dws", "dv", "dout", "left"] + \
    ["a%s%d" % (k, t) for k in "plh" for t in range(ROUNDS)]


def bits(engs):
    return sum(1 << e for e in engs)


def routes(T, topo, t, kind, r):
    src = T.cores[r]
    dst = T.cores[(r - 1 - t) % N] if kind == "p" else T.cores[(r + 1 + t) % N]
    q, s, a = ("tq%d" % t, "ts%d" % t, 240) if kind == "p" else ("hq%d" % t, "hs%d" % t, 112)
    codes = (lambda: T[q][:, a:a + K].bitcast(dt.uint8)), (lambda: T[q][:, 0:K].bitcast(dt.uint8))
    plane = (lambda: T[s][:, a:a + K]), (lambda: T[s][:, 0:K])
    lst = (lambda: T["lo%d" % t][:]), (lambda: T["li%d" % t][:])
    if topo.may_write(src, dst) and (t, kind) != (0, "p"):
        e = topo.engines(src, dst)
        if kind == "l":
            return dst, [lst + (None, e, None)]
        return dst, [codes + (None, e, None), plane + (None, e, None)]
    able = [c for c in topo.cores_of(src) if all(topo.may_write(c, d) for d in T.cores)]
    near = [c for c in able if topo.die(c) == topo.die(src)][0]
    far = [c for c in able if topo.die(c) != topo.die(src)][0]
    e = topo.engines(src, near)
    if kind == "l":
        return dst, [lst + (near, e, topo.engines(near, dst))]
    return dst, [codes + (near, e, topo.engines(near, dst)), plane + (far, e, topo.engines(far, dst))]


def landing(T, topo, t, kind, r):
    s = (r + 1 + t) % N if kind == "p" else (r - 1 - t) % N
    return sum(len(p[4] if p[2] is not None else p[3]) for p in routes(T, topo, t, kind, s)[1])


def relay_program(g, core, T, topo):
    left = 0
    for t in range(ROUNDS):
        for kind in "plh":
            for r in range(N):
                dst, pieces = routes(T, topo, t, kind, r)
                for _, land, via, e1, e2 in pieces:
                    if via == core:
                        sem = T.sem["a%s%d" % (kind, t)]
                        g.wait_ge(sem, len(e1))
                        rid, pid = topo.addr(dst, core)
                        g.remote_dma(land(), land(), sem, T.sem.left, pid, rid, bits(e2))
                        left += len(e2)
    if left:
        g.wait_ge(T.sem.left, left)


def rank_program(g, core, T, topo):
    rank = T.rank_of(core)
    if rank is None:
        relay_program(g, core, T, topo)
        return
    Q = {"V": g.vector, "A": g.scalar, "P": g.tensor, "G": g, "S": g.sync}
    V, A, P = g.vector, g.scalar, g.tensor
    total, seen, wrote, readers = {}, {e: {} for e in Q}, {}, {}

    def need(e, r, w):
        tok = []
        for k in r:
            if k in wrote:
                tok.append(wrote[k])
            if k.startswith("ps"):
                tok += [x for x in readers.get(k, []) if x[0] != "c" + e]
        for k in w:
            if k in wrote:
                tok.append(wrote[k])
            tok += readers.get(k, [])
        most = {}
        for s, n in tok:
            most[s] = max(most.get(s, 0), n)
        for s, n in most.items():
            if seen[e].get(s, 0) < n:
                Q[e].wait_ge(T.sem[s], n)
                seen[e][s] = n

    def op(e, call, r, w, sem=None):
        need(e, r, w)
        s, n = ("c" + e, 1) if sem is None else (sem, 16)
        call().then_inc(T.sem[s], n)
        total[s] = total.get(s, 0) + n
        for k in r:
            readers.setdefault(k, []).append((s, total[s]))
        for k in w:
            wrote[k], readers[k] = (s, total[s]), []

    def send(t, kind, r):
        need("G", r, [])
        dst, pieces = routes(T, topo, t, kind, rank)
        for src, land, via, e1, _ in pieces:
            rid, pid = topo.addr(dst if via is None else via, core)
            g.remote_dma(land(), src(), T.sem["a%s%d" % (kind, t)], T.sem.left, pid, rid, bits(e1))
        total["left"] = total.get("left", 0) + sum(len(p[3]) for p in pieces)

    for t in range(ROUNDS):
        for kind in "plh":
            s = "a%s%d" % (kind, t)
            total[s] = landing(T, topo, t, kind, rank)
            wrote[s] = (s, total[s])

    def bank(i, a, b):
        return T.ps[:, 512 * i + a:512 * i + b]

    def mm(i, lq, ls, l0, rq, rs, a, b, r):
        op("P", lambda: P.matmul_mx(bank(i, 0, b - a), lq[:, l0:l0 + 128], ls[:, l0:l0 + 128], rq[:, a:b], rs[:, a:b],
                                    True, True), r, ["ps%d" % i])

    def cp(e, out, in_, r, w):
        if e == "V":
            op(e, lambda: V.tensor_copy(out, in_), r, w)
        else:
            op(e, lambda: A.activation(out, in_, Act.Copy), r, w)

    def fill(ap, c, w):
        op("V", lambda: V.memset(ap, c), [], w)

    def afill(ap, n, c, w):
        op("A", lambda: A.activation(ap, T.zer[:, 0:n], Act.Identity, bias=c), ["zer"], w)

    def iota(ap, pat, base, mul, w, whole=False):
        if whole:
            op("G", lambda: g.iota(ap, pat, base, mul), [], w)
        else:
            op("G", lambda: g.iota(ap, pat, base, mul, allow_small_or_imprecise_dtypes=True), [], w)

    def ts(out, in0, s1, s2, o0, o1, r, w):
        if o1 is None:
            op("V", lambda: V.tensor_scalar(out, in0, s1, None, o0), r, w)
        else:
            op("V", lambda: V.tensor_scalar(out, in0, s1, s2, o0, o1), r, w)

    def tt(out, in0, in1, o, r, w):
        op("V", lambda: V.tensor_tensor(out, in0, in1, o), r, w)

    def scan(out, d0, d1, init, o0, o1, r, w):
        op("V", lambda: V.tensor_tensor_scan(out, d0, d1, init, o0, o1), r, w)

    def quant(q, s, a, b, in_, r, w):
        op("V", lambda: V.quantize_mx(q[:, a:b], s[:, a:b], in_), r, w)

    def level(blk, k):
        o, d0, src, prev = {"O": (0, T.sc[:, 1:C:2], "scO", None), "E": (K, bank(5, 0, K), "ps5", "O"),
                            "P": (C, bank(4, 0, K), "ps4", "E")}[blk]
        b = k * RW + o
        d1 = T.big[:] if k == 0 else T.rr[:, b - RW:b - RW + K]
        rd = [src, "big", "r0"] + ["r%s%d" % (x, k - 1) for x in (blk, prev) if x and k]
        if prev:
            rd.append("r%s%d" % (prev, k))
        scan(T.rr[:, b + 1:b + 1 + K], d0, d1, T.rr[:, b:b + 1], Alu.max, Alu.min, rd, ["r%s%d" % (blk, k)])

    def best(blk, a, b=None):
        col = C if blk == "E" else RW - 1
        return T.rr[:, a * RW + col:(a if b is None else b) * RW + col + 1:RW]

    def same(blk, a, b):
        o, a = (0 if blk == "E" else 8), max(a, 1)
        tt(T.ej[:, o + a:o + b + 1], best(blk, a, b), best(blk, a - 1, b - 1), Alu.is_equal,
           ["r%s%d" % (blk, k) for k in range(a - 1, b + 1)], ["ej%s%d" % (blk, b)])

    def number(blk, a, b):
        o = 0 if blk == "E" else 8
        scan(T.nj[:, o + a:o + b + 1], T.ej[:, o + a:o + b + 1], T.mu[:, a:b + 1], T.nj[:, o + a - 1:o + a] if a else 0.0,
             Alu.mult, Alu.add, ["ej%s%d" % (blk, b), "ej0", "mu"] + ["nj%s%d" % (blk, a - 1)] * (a > 0),
             ["nj%s%d" % (blk, k) for k in range(a, b + 1)])

    def differ(seg):
        c = seg if seg < 7 else 8 + seg % 7
        lst, key = (T.ll, "ll") if seg < 14 else (T.lg, "lg")
        ts(T.dd[:, seg * DW:seg * DW + K], lst[:], T.ids[:, c:c + 1], 512.0, Alu.not_equal, Alu.mult, [key, "ids"],
           ["dd%d" % seg])

    def first_hit(blk):
        a, b = 7 * blk * DW, 7 * (blk + 1) * DW
        scan(T.do[:, a:b], T.dd[:, a:b], T.rm[:], 4096.0, Alu.min, Alu.add,
             ["dd%d" % s for s in range(7 * blk, 7 * blk + 7)] + ["ddr", "ddx", "rm"], ["do%d" % blk])

    def hits(blk, x=0):
        return T.do[:, 7 * blk * DW + K - 1 + x:7 * (blk + 1) * DW:DW]

    op("S", lambda: g.sync.dma_start(T.xin[:], T.x[:]), [], ["xin"], "dx")
    iota(T.idb[:], [[1, 128]], 0, -1, ["idb"])
    iota(T.pi[:, 0:1], [[1, 1]], 0, 1, ["pi0"], True)
    iota(T.c15[:], [[16, 15]], 112 - 176, 0, ["c15"])
    iota(T.apart[:], [[-C, 8]], 7 * C, 0, ["apart"])
    fill(T.zer[:], 0.0, ["zer"])
    fill(T.xs[:, 448:512], 0.0, ["xpO"])
    fill(T.xs[:, 960:1024], 0.0, ["xpE"])
    fill(T.un[:], 0.0, ["un"])
    afill(T.rr[:, 0:8 * RW:RW], 8, -BIG, ["r0"])
    afill(T.big[:], K, BIG, ["big"])
    afill(T.one[:], C, 1.0, ["one"])
    afill(T.mu[:], 8, -UNIT, ["mu"])
    afill(T.ej[:, 0:16:8], 2, 0.0, ["ej0"])
    afill(T.tb[:, 8:9], 1, 0.0, ["tb8"])
    afill(T.e2[:, 7 * CW:7 * CW + 1], 1, -UNIT, ["e2x"])
    afill(T.dd[:, K:21 * DW:DW], 21, 512.0, ["ddx"])
    afill(T.dd[:, K + 1:21 * DW:DW], 21, 512.0, ["ddr"])
    afill(T.rm[:], 7 * DW, -1.0, ["rm"])
    fill(T.zt[:, 448:512], 0.0, ["zp"])
    fill(T.ht[:, 448:512], 0.0, ["hp"])
    for b in range(4):
        ts(T.un[:, 512 * b + b:512 * b + 512:4], T.idb[:], 0.0, None, Alu.is_equal, None, ["idb", "un"], ["un%d" % b])
    op("A", lambda: A.activation(T.mk[:], T.un[:, 0:4 * K:4], Act.Copy, scale=-1.0e29), ["un0"], ["mk"])
    afill(T.rm[:, K:7 * DW:DW], 7, 128.0, ["rm"])
    cp("A", T.c1[:, C:8 * CX:CX], T.apart[:], ["apart"], ["c1x"])
    afill(T.rm[:, K + 1:7 * DW:DW], 7, 4096.0, ["rm"])

    XO, XE = ["xO%d" % b for b in range(4)], ["xE%d" % b for b in range(4)]
    for b in range(4):
        cp("V", T.xs[:, 512 + b:960:4], T.xin[:, b:4 * C:8], ["xin"], [XE[b]])
    for b in range(4):
        cp("V", T.xs[:, b:448:4], T.xin[:, 4 + b:4 * C:8], ["xin"], [XO[b]])

    def odd_scores(t):
        tq, tsc = T["tq%d" % t], T["ts%d" % t]
        quant(tq, tsc, 112, 240, T.xs[:, 0:512], XO + ["xpO"], ["tO%d" % t])
        mm(4, tq, tsc, 112, tq, tsc, 112, 240, ["tO%d" % t])

    def odd_mask():
        tt(T.sc[:, 1:C:2], bank(4, 0, K), T.mk[:], Alu.add, ["ps4", "mk"], ["scO"])

    for t in range(ROUNDS):
        last = t == ROUNDS - 1
        tq, tsc, hq, hs = T["tq%d" % t], T["ts%d" % t], T["hq%d" % t], T["hs%d" % t]
        off, kL = T["lo%d" % t], "lo%d" % t
        kO, kE, kP, kH, kG = "tO%d" % t, "tE%d" % t, "ap%d" % t, "hH%d" % t, "ah%d" % t
        quant(tq, tsc, 240, W, T.xs[:, 512:1024], XE + ["xpE"], [kE])
        send(t, "p", [kE])
        if t == 0:
            odd_scores(0)
            ts(T.pi[:, 1:2], T.pi[:, 0:1], 15, None, Alu.bitwise_and, None, ["pi0"], ["pi1"])
            quant(T.eq, T.es, 0, 512, T.un[:], ["un%d" % b for b in range(4)], ["eq"])
            odd_mask()
            cp("V", T.pf[:], T.pi[:, 1:2], ["pi1"], ["pf"])
            for b in range(4):
                fill(T.ep[:, 256 * b + 240:256 * b + 256], 0.0, ["ez%d" % b])
            level("O", 0)
            ts(T.dl[:, 8:CW], T.zer[:, 0:K], 1.0, None, Alu.add, None, ["zer"], ["dlc"])
            ts(T.ids[:], T.c15[:], T.pf[:], None, Alu.add, None, ["c15", "pf"], ["ids"])
            level("O", 1)
            iota(T.sl[:, 0:K + 1], [[-1, K + 1]], K - 176, 0, ["sl0"])
            iota(T.sl[:, K + 1:NS], [[0, 8], [-1, K], [128, 2]], 223 - 176, 0, ["sl1"])
            iota(T.idc[:], [[1, VW]], -176, 0, ["idc"])
            iota(T.idg[:, 0:K], [[1, K]], 240 - 176, 0, ["idg0"])
            afill(T.idg[:, K:VW], VW - K, -200.0, ["idg1"])
        if t == 1:
            iota(T.pls[:, 0:112], [[1, K]], C, 0, ["pl0"])
            iota(T.pls[:, 112:240], [[2, 128]], 1, 0, ["pl1"])
            iota(T.pls[:, 240:VW], [[2, K]], 0, 0, ["pl2"])
        mm(5, tq, tsc, 112, tq, tsc, 240, W, [kO, kE])
        mm(6, tq, tsc, 112, tq, tsc, 240, W, [kO, kE])
        cp("A", T.sc[:, 0:C:2], bank(6, 0, K), ["ps6"], ["scE"])
        apart = set()

        def aside():
            if t == 1:
                quant(T.vq, T.vs, 0, 128, T.vin[:], ["vin"], ["vq"])

        def loads():
            if t == 0:
                op("S", lambda: g.sync.dma_start(T.wq[:].bitcast(dt.uint8), T.wc[:]), ["rE6"], ["wq"], "dwc")
                op("S", lambda: g.sync.dma_start(T.wp[:], T.ws[:]), [], ["wp"], "dws")
                op("S", lambda: g.sync.dma_start(T.vin[:], T.v[:]), [], ["vin"], "dv")

        def distance(k):
            apart.add(k)
            op("A", lambda: A.activation(T.d1[:, k * C:(k + 1) * C], T.sc[:], Act.Identity, bias=best("E", k),
                                         scale=-1.0), ["scO", "scE", "rE%d" % k], ["d1%d" % k])

        def own_equal(k):
            out = T.e1[:, k * C:(k + 1) * C]
            if k in apart:
                ts(out, T.d1[:, k * C:(k + 1) * C], 0.0, HIT, Alu.is_equal, Alu.mult, ["d1%d" % k], ["e1%d" % k])
            else:
                ts(out, T.sc[:], best("E", k), HIT, Alu.is_equal, Alu.mult, ["scO", "scE", "rE%d" % k], ["e1%d" % k])

        def own_count(k):
            scan(T.c1[:, k * CX:k * CX + C], T.e1[:, k * C:(k + 1) * C], T.one[:], T.nj[:, k:k + 1], Alu.add, Alu.min,
                 ["e1%d" % k, "one", "njE%d" % k], ["c1%d" % k])

        def own_name(k):
            op("A", lambda: A.activation(T.s1[:, k * CX:(k + 1) * CX], T.c1[:, k * CX:(k + 1) * CX], Act.Relu,
                                         accum_out=T.tb[:, k:k + 1]), ["c1%d" % k, "c1x"], ["tb%d" % k, "s1%d" % k])

        def partner_level(k):
            if k == 0:
                mm(4, tq, tsc, 112, tq, tsc, 0, 128, [kO, kP])
                mm(7, tq, tsc, 112, tq, tsc, 0, 128, [kO, kP])
                for b in range(4):
                    mm(b, T.eq, T.es, 128 * b, tq, tsc, 0, VW, ["eq", kO, kE, kP])
            level("P", k)
            if k == 0:
                cp("A", T.cn[:, 8:CW], bank(7, 0, K), ["ps7"], ["cn1"])

        def own_values():
            cp("V", T.cn[:, 0:8], best("E", 0, 7), ["rE%d" % k for k in range(8)], ["cn0"])

        def steps():
            tt(T.dl[:, 0:8], T.tb[:, 0:8], T.tb[:, 1:9], Alu.subtract, ["tb%d" % k for k in range(9)], ["dl"])

        def values(b):
            cp("A", T.vp[:, VW * b:VW * (b + 1)], bank(b, 0, VW), ["ps%d" % b], ["vp%d" % b])

        def far(k):
            apart.add(8 + k)
            op("A", lambda: A.activation(T.d2[:, k * CW:(k + 1) * CW], T.cn[:], Act.Identity, bias=best("P", k),
                                         scale=-1.0), ["cn0", "cn1", "rP%d" % k], ["d2%d" % k])

        def seg(buf, k):
            return buf[:, k * CW + k // 7:(k + 1) * CW + k // 7]

        def slot(k):
            return 3 * (k % 2) + k // 2 if k < 6 else 18 + k

        def equal(k):
            if k == 0:
                ts(seg(T.c2, 0), T.cn[:], best("P", 0), -UNIT, Alu.not_equal, Alu.mult, ["cn0", "cn1", "rP0"], ["c20"])
            elif 8 + k in apart:
                ts(seg(T.e2, k), T.d2[:, k * CW:(k + 1) * CW], 0.0, UNIT, Alu.is_equal, Alu.mult, ["d2%d" % k],
                   ["e2%d" % k])
            else:
                ts(seg(T.e2, k), T.cn[:], best("P", k), UNIT, Alu.is_equal, Alu.mult, ["cn0", "cn1", "rP%d" % k],
                   ["e2%d" % k])

        def last_number():
            ts(T.nj[:, 15:16], best("P", 7), best("P", 6), T.nf[:, 2:3], Alu.is_equal, Alu.mult,
               ["rP6", "rP7", "nf"], ["njP7"])

        def wide_numbers():
            scan(T.nf[:], T.ej[:, 12:15], T.mu[:, 0:3], T.nj[:, 11:12], Alu.mult, Alu.add, ["ejP6", "mu", "njP3"], ["nf"])

        def count(k):
            a, b = k * CW, (k + 1) * CW + k // 7
            scan(T.c2[:, a:b], T.e2[:, a:b], T.zer[:, 0:b - a], T.nj[:, 8 + k:9 + k], Alu.add, Alu.min,
                 ["e2%d" % k, "e2x", "zer", "njP%d" % k], ["c2%d" % k])

        def name(k):
            scan(T.s2[:, slot(k) * CW:(slot(k) + 1) * CW], seg(T.c2, k), T.dl[:], -8 * UNIT, Alu.max, Alu.add,
                 ["c2%d" % k, "dl", "dlc"], ["s2%d" % k])

        def gather_names():
            for a in range(1, 4):
                cp("V", T.s2[0:32, (6 * a + 1) * CW - 1:6 * (a + 1) * CW:CW], T.s2[32 * a:32 * a + 32, CW - 1:6 * CW:CW],
                   ["s2%d" % k for k in range(6)], ["m2%d" % a])

        def deal_names():
            for h in range(3):
                cp("V", T.mh[32 * h:32 * h + 32, :], T.s2[0:32, (h + 1) * CW - 1:24 * CW:3 * CW],
                   ["s2%d" % k for k in range(6)] + ["m21", "m22", "m23"], ["mh%d" % h])

        def move_names(h):
            for a in range(4):
                cp("V", T.mh[32 * h:32 * h + 32, 2 * a:2 * a + 2],
                   T.s2[32 * a:32 * a + 32, (slot(2 * h) + 1) * CW - 1:(slot(2 * h) + 2) * CW:CW],
                   ["s2%d" % (2 * h), "s2%d" % (2 * h + 1)], ["mh%d%d" % (h, a)])

        words = {"-": aside, "cx": loads, "cn": own_values, "dl": steps, "y7": last_number, "y6": wide_numbers, "two": gather_names,
                 "one": deal_names, "four2": lambda: move_names(2), "four3": lambda: move_names(3)}
        calls = {"O": lambda k: level("O", k), "E": lambda k: level("E", k), "P": partner_level, "d": distance,
                 "q": own_equal, "c": own_count, "a": own_name, "D": far, "v": values, "n": equal, "t": count, "m": name,
                 "j": lambda a, b: same("E", a, b), "J": lambda a, b: number("E", a, b),
                 "k": lambda a, b: same("P", a, b), "K": lambda a, b: number("P", a, b)}
        wave = WAVE
        if t == 0:
            wave = sorted(WAVE, key=lambda x: x[0] not in "OE-qcajJd" or x in ("dl", "c6", "c7", "a6", "a7"))
        for word in wave:
            if word in words:
                words[word]()
            else:
                calls[word[0]](*[int(x) for x in word[1:]])

        cp("V", T.bb[:], T.sl[:].indirect(T.mh[:]),
           ["mh0", "mh1", "mh2", "sl0", "sl1"] + ["mh3%d" % a for a in range(4)], ["bb"])
        op("V", lambda: V.transpose(T.tt[:], T.bb[:]), ["bb"], ["tt"])
        ts(off[:], T.tt[:, 0:128:16], 176.0, None, Alu.add, None, ["tt"], [kL])
        send(t, "l", [kL])
        for b in (0, 2, 1, 3):
            cp("VVAA"[b], T.zt[:, b:448:4], T.vp[:, VW * b:VW * (b + 1)].indirect(off[:, 0:7]), [kL, "vp%d" % b],
               ["z%d" % b])
        cp("V", T.ll[:], T.idc[:].indirect(off[:, 0:7]), [kL, "idc"], ["ll"])
        quant(T.zq, T.zs, 0, 128, T.zt[:], ["z0", "z1", "z2", "z3", "zp"], ["zq"])
        for b in (0, 2, 1, 3):
            mm(4 + b, T.wq, T.wp, 128 * b, T.zq, T.zs, 0, 128, ["wq", "wp", "zq"])
        for s in range(10):
            differ(s)
        for b in (0, 2, 1, 3):
            if b < 2:
                ts(T.ht[:, b:448:4], bank(4 + b, 0, K), 0.03125, None, Alu.mult, None, ["ps%d" % (4 + b)], ["h%d" % b])
            else:
                op("A", lambda: A.activation(T.ht[:, b:448:4], bank(4 + b, 0, K), Act.Copy, scale=0.03125),
                   ["ps%d" % (4 + b)], ["h%d" % b])
        for s in range(10, 14):
            differ(s)
        quant(hq, hs, 112, 240, T.ht[:], ["h0", "h1", "h2", "h3", "hp"], [kH])
        send(t, "h", [kH])
        for b in range(4):
            mm(b, T.eq, T.es, 128 * b, hq, hs, 112, 240, ["eq", kH])
        mm(5, T.eq, T.es, 384, tq, tsc, 240, W, ["eq", kE])
        cp("A", T.lg[:], T.idg[:].indirect(T["li%d" % t][:, 0:7]), ["al%d" % t, "idg0", "idg1"], ["lg"])
        for b in range(4):
            cp("A", T.ep[:, 256 * b:256 * b + 128], bank(b, 0, 128), ["ps%d" % b], ["eo%d" % b])
        first_hit(0)
        first_hit(1)
        ts(T.oo[:, 0:7], hits(0), 0.0, 112.0, Alu.min, Alu.add, ["do0"], ["oo"])
        for s in range(14, 21):
            differ(s)
        for b in range(4):
            out = T.xf[:, 4 + b:4 * C:8] if last else T.xs[:, b:448:4]
            tt(out, T.ep[:, 256 * b:256 * b + 128].indirect(T.oo[:, 0:7]), T.vp[:, VW * b + 112:VW * b + 224], Alu.add,
               ["oo", "eo%d" % b, "vp%d" % b], [XO[b]])
        first_hit(2)
        if last:
            cp("A", T.opb[:], T.pls[:].indirect(off[:, 0:7]), [kL, "pl0", "pl1", "pl2"], ["opb"])
            for k in range(8):
                op("S", lambda: g.sync.dma_start(T.op[k:k + 1, :], T.opb[16 * k:16 * k + 1, :]), ["opb"], [], "dout")
        else:
            odd_scores(t + 1)
        tt(T.mn[:, 0:7], hits(1), hits(2, 1), Alu.min, ["do1", "do2"], ["mn"])
        ts(T.oe[:, 0:7], T.mn[:, 0:7], 128.0, 112.0, Alu.min, Alu.add, ["mn"], ["oe"])
        if not last:
            odd_mask()
        for b in (0, 3, 1, 2):
            mm(b, T.eq, T.es, 128 * b, hq, hs, 0, 128, ["eq", kH, kG])
        for b in (0, 3, 1, 2):
            cp("AVAA"[b], T.ep[:, 256 * b + 128:256 * b + 240], bank(b, 0, K), ["ps%d" % b], ["eg%d" % b])
        cp("A", T.ga[:], T.ep[:, 768:1024].indirect(T.oe[:, 0:7]), ["oe", "eo3", "eg3", "ez3"], ["ga"])
        for b in range(4):
            out = T.xf[:, b:4 * C:8] if last else T.xs[:, 512 + b:960:4]
            if b == 3:
                tt(out, T.ga[:], bank(5, 0, K), Alu.add, ["ga", "ps5"], [XE[b]])
                continue
            tt(out, T.ep[:, 256 * b:256 * b + 256].indirect(T.oe[:, 0:7]), T.vp[:, VW * b + 240:VW * b + 352], Alu.add,
               ["oe", "eo%d" % b, "eg%d" % b, "ez%d" % b, "vp%d" % b], [XE[b]])
            if b == 0 and not last:
                level("O", 0)
        if not last:
            level("O", 1)

    quant(T.fq, T.fs, 0, C, T.xf[:], XO + XE, ["fq"])
    mm(4, T.vq, T.vs, 0, T.fq, T.fs, 0, C, ["vq", "fq"])
    op("S", lambda: g.sync.dma_start(T.oc[:], T.fq[:].bitcast(dt.uint8)), ["fq"], [], "dout")
    for k in range(4):
        op("A", lambda: A.dma_start(T.osc[4 * k:4 * k + 4, :], T.fs[32 * k:32 * k + 4, :]), ["fq"], [], "dout")
    cp("V", T.yo[:], bank(4, 0, C), ["ps4"], ["yo"])
    op("S", lambda: g.sync.dma_start(T.y[:], T.yo[:]), ["yo"], [], "dout")
    for s, n in total.items():
        g.wait_ge(T.sem[s], n)
